import numpy as np
import ml_dtypes


def mxq(x, axis, fmt="e4m3"):
    dtype, down = {"e4m3": (ml_dtypes.float8_e4m3fn, 7), "e5m2": (ml_dtypes.float8_e5m2, 14)}[fmt]
    v = np.moveaxis(np.asarray(x, np.float32).astype(ml_dtypes.bfloat16).astype(np.float64), axis, -1)
    blocks = v.reshape(v.shape[:-1] + (-1, 32))
    amax = np.abs(blocks).max(-1, keepdims=True)
    byte = np.maximum(np.where(amax > 0, np.frexp(amax)[1] - 1 + 127, 0) - down, 1)
    scale = np.exp2(byte - 127.0)
    codes = (blocks / scale).astype(np.float32).astype(dtype).astype(np.float64)
    return np.moveaxis((codes * scale).reshape(v.shape), -1, axis)


WIDE = False


def mx_kscale(k):
    if not WIDE:
        return np.ones(k)
    levels = np.array([10, -10, 5, -5, 0])
    if k % 512:
        return np.exp2(np.random.permutation(np.resize(levels, k // 32))).repeat(32)
    a = np.empty((k // 512, 16))
    for p in range(k // 512):
        a[p, :8] = np.random.permutation(np.resize(levels, 8))
        for g in range(8):
            far = levels[np.abs(levels - a[p, g]) >= 10]
            a[p, g + 8] = far[np.random.randint(len(far))]
    return np.exp2(a.ravel()).repeat(32)


def f64(x):
    return np.asarray(x).astype(np.float64)


def striped(idx):
    return np.tile(np.asarray(idx).reshape(-1, 16).T, (8, 1)).astype(np.uint16)


def unstriped(offs):
    return offs[:16].T.reshape(-1).astype(np.int64)


E2M1 = np.array([0.0, 0.5, 1.0, 1.5, 2.0, 3.0, 4.0, 6.0, -0.0, -0.5, -1.0, -1.5, -2.0, -3.0, -4.0, -6.0])


def pack_weight(w, fmt):
    k, n = w.shape
    w = f64(np.asarray(w, np.float32).astype(ml_dtypes.bfloat16)).reshape(k // 32, 32, n)
    amax = np.abs(w).max(1)
    if fmt == "e4m3":
        byte = np.frexp(amax)[1] - 1 + 127 - 7
    else:
        mant, ex = np.frexp(amax / 6.0)
        byte = np.where(mant > 0.5, ex, ex - 1) + 127
    byte = np.clip(np.where(amax > 0, byte, 1), 1, 254)
    scaled = (w * np.exp2(127.0 - byte)[:, None, :]).reshape(k, n).astype(np.float32)
    by_word = np.ascontiguousarray(scaled.reshape(k // 512, 128, 4, n).transpose(0, 1, 3, 2))
    if fmt == "e4m3":
        words = by_word.astype(ml_dtypes.float8_e4m3fn).view(np.uint8)
    else:
        c = by_word.astype(ml_dtypes.float4_e2m1fn).view(np.uint8) & 0xF
        words = (c[..., 0::2] | (c[..., 1::2] << 4)).reshape(k // 512, 128, 2 * n)
    return np.ascontiguousarray(words), np.ascontiguousarray(byte.astype(np.uint8).reshape(k // 512, 16, n))


def unpack_weight(words, scales, fmt):
    g, _, n = scales.shape
    words = np.ascontiguousarray(words).reshape(g, 128, n, -1)
    if fmt == "e4m3":
        vals = words.view(ml_dtypes.float8_e4m3fn).astype(np.float64)
    else:
        nib = np.empty((g, 128, n, 4), np.uint8)
        nib[..., 0::2] = words & 0xF
        nib[..., 1::2] = words >> 4
        vals = E2M1[nib]
    vals = vals * np.repeat(np.exp2(scales.astype(np.float64) - 127.0), 8, axis=1)[..., None]
    return vals.transpose(0, 1, 3, 2).reshape(g * 512, n)


def bf(x):
    return np.asarray(x, np.float32).astype(ml_dtypes.bfloat16)


def planes(Y):
    r, m = Y.shape
    b = f64(bf(Y)).reshape(r // 32, 32, m)
    amax = np.abs(b).max(1)
    byte = np.clip(np.where(amax > 0, np.frexp(amax)[1] - 1 + 127 - 7, 1), 1, 254)
    codes = (b * np.exp2(127.0 - byte)[:, None, :]).reshape(r, m).astype(np.float32).astype(ml_dtypes.float8_e4m3fn).view(np.uint8)
    words = codes.reshape(r // 512, 128, 4, m).transpose(0, 1, 3, 2)
    return np.ascontiguousarray(words), np.ascontiguousarray(byte.astype(np.uint8).reshape(r // 512, 16, m))


B, N, T, D, NQ = 1, 512, 2048, 1024, 512


def setup_inputs():
    n = np.random.standard_normal
    idx = np.random.permutation(T)[:B * N]
    s = mx_kscale(D)[:, None]
    kp = pack_weight(n((D, T)) / s, "e2m1")
    return {
        "qT": (n((B, D, NQ)) * s * (1.00 / np.sqrt(D))).astype(np.float32),
        "k_words": np.ascontiguousarray(kp[0].reshape(1, 2, 128, T, 2).transpose(0, 2, 3, 1, 4)).reshape(1, 128, T, 4),
        "k_scales": kp[1],
        "kb": np.tile(n(2048), (128, 1)).astype(np.float32),
        "ls": (np.random.uniform(7.8, 8.4, (B, NQ, 1))).astype(np.float32),
        "offs": striped(idx),
    }


def reference(qT, k_words, k_scales, kb, ls, offs):
    idx = unstriped(offs)
    pick = lambda x, which: x[:, which].reshape(x.shape[0], B, -1).transpose(1, 0, 2)
    k = unpack_weight(k_words.reshape(1, 128, T, 2, 2).transpose(0, 3, 1, 2, 4).reshape(2, 128, 2 * T), k_scales, "e2m1")
    kg = pick(k, idx)
    qq = mxq(f64(qT), 1, "e4m3")
    a = qq.transpose(0, 2, 1) @ kg
    y = np.exp(a + pick(f64(kb), idx)[:, :1, :] - f64(ls))
    Y = y[0]
    words, scales = planes(Y)
    return Y, words, scales

@@ -1,0 +1,149 @@
+from contextlib import ExitStack
+
+import concourse.mybir as mybir
+from concourse.masks import make_identity
+
+F32 = mybir.dt.float32
+BF16 = mybir.dt.bfloat16
+I32 = mybir.dt.int32
+U32 = mybir.dt.uint32
+U16 = mybir.dt.uint16
+U8 = mybir.dt.uint8
+FP8X4 = mybir.dt.float8_e4m3fn_x4
+FP4X4 = mybir.dt.float4_e2m1fn_x4
+ACT = mybir.ActivationFunctionType
+ALU = mybir.AluOpType
+
+P = 128
+PACK = 4
+N, T, D, NQ = 512, 2048, 1024, 512
+PASSES = D // (P * PACK)
+FLOPS = 2 * NQ * N * D
+
+HALF = N // 2
+
+
+def tile_attend_plq_recomp_topk_kernel(tc, qT, k_words, k_scales, kb, ls, offs, out_0, out_1, out_2):
+    nc = tc.nc
+    with ExitStack() as ctx:
+        keep = ctx.enter_context(tc.tile_pool(name="keep", bufs=1))
+        psum = ctx.enter_context(tc.psum_pool(name="psum", bufs=1))
+
+        q_rows = qT[0].rearrange("(g p j) q -> g p j q", g=PASSES, j=PACK)
+
+        offsets = keep.tile([P, N // 16], U16, name="offsets")
+        nc.sync.dma_start(offsets[:], offs)
+        scale_pool = keep.tile([P, T], U8, name="scale_pool", tag="q_rest", align_bytes=64)
+        scale_words = scale_pool[:].bitcast(I32)
+        nc.sync.dma_start(scale_words[96:128, :], k_scales.bitcast(I32).rearrange("o f t -> f o t"))
+        q_first = keep.tile([P, 2, NQ], F32, name="q_first")
+        nc.sync.dma_start(q_first[:], q_rows[0, :, 0:2, :])
+        word_pool = keep.tile([P, T], I32, name="word_pool", align_bytes=64)
+        nc.sync.dma_start(word_pool[:], k_words[0].rearrange("p t b -> p (t b)").bitcast(I32))
+
+        warm_in = keep.tile([P, 1], F32, name="warm_in")
+        warm_out = keep.tile([P, 1], F32, name="warm_out")
+        nc.gpsimd.memset(warm_in[:], 0.0)
+        nc.scalar.activation(warm_out[:], warm_in[:], ACT.Exp)
+
+        bias_pool = keep.tile([P, T], F32, name="bias_pool", tag="bias_pool", align_bytes=64)
+        nc.vector.memset(bias_pool[:], 0.0)
+        nc.scalar.dma_start(bias_pool[0:1, :], kb[0:1, :])
+        nc.vector.memset(scale_words[0:96, :], 0)
+
+        k_planes = keep.tile([P, PASSES * N], U8, name="k_planes", align_bytes=64)
+        nc.gpsimd.memset(k_planes[:].bitcast(I32), 0)
+        ident = keep.tile([P, P], F32, name="ident")
+        make_identity(nc, ident[:])
+        lse = keep.tile([P, PACK], F32, name="lse")
+        nc.gpsimd.dma_start(lse[:], ls[0].rearrange("(p u) o -> p (u o)", u=PACK))
+
+        k_rows = keep.tile([P, N], U8, name="k_rows", align_bytes=64)
+        nc.vector.tensor_copy(k_rows[:], scale_pool[:].indirect(offsets[:]))
+        q_rest = keep.tile([P, 6, NQ], F32, name="q_rest", tag="q_rest", align_bytes=64)
+        q_second, q_last = q_rest[:, 0:2, :], q_rest[:, 2:6, :]
+        nc.sync.dma_start(q_second, q_rows[0, :, 2:4, :])
+        for quad in range(4):
+            nc.sync.dma_start(k_planes[:].bitcast(I32)[32 * quad:32 * quad + 4, :],
+                              k_rows[:].bitcast(I32)[96 + 8 * quad:96 + 8 * quad + 8, :])
+        nc.sync.dma_start(q_last, q_rows[1])
+
+        bias_row = keep.tile([P, N], F32, name="bias_row", align_bytes=64)
+        nc.vector.tensor_copy(bias_row[:], bias_pool[:].indirect(offsets[:]))
+
+        k_pairs = keep.tile([P, N], U32, name="k_pairs", tag="bias_pool", align_bytes=64)
+        nc.vector.tensor_copy(k_pairs[:], word_pool[:].bitcast(U32).indirect(offsets[:]))
+        halves = k_pairs[:].bitcast(U16).rearrange("p (i h) -> p h i", h=2)
+
+        turned = psum.tile([P, N // P, P], F32, name="turned")
+        for s in range(N // P):
+            nc.tensor.transpose(turned[:, s, :], bias_row[:, s * P:(s + 1) * P], ident[:])
+        bias_cols = keep.tile([P, N // P], F32, name="bias_cols")
+        nc.scalar.copy(bias_cols[:], turned[:, :, 0])
+        spread = psum.tile([P, N], F32, name="spread")
+        for s in range(N // P):
+            nc.tensor.transpose(spread[:, s * P:(s + 1) * P], bias_cols[:, s:s + 1].to_broadcast([P, P]), ident[:])
+        bias_all = keep.tile([P, N], F32, name="bias_all")
+        nc.scalar.copy(bias_all[:], spread[:])
+
+        def deal(engine, grouped, raw, j0, u0):
+            rows, count = raw.shape[1], grouped.shape[1]
+            src = raw.rearrange("p j (m u) -> p m j u", u=PACK)[:, :, :, u0:u0 + count]
+            dst = grouped[:].rearrange("p u m j -> p m j u")[:, :, j0:j0 + rows, :]
+            engine(dst, src)
+
+        scores = [psum.tile([P, N], F32, name="scores%d" % u) for u in range(PACK)]
+        for g in range(PASSES):
+            k_codes = keep.tile([P, N], U16, name="k_codes%d" % g, align_bytes=64)
+            nc.vector.tensor_copy(k_codes[:], halves[:, g, :])
+            split = 2 if g == 0 else 3
+            low = keep.tile([P, split, P, PACK], BF16, name="q_low%d" % g, align_bytes=64)
+            high = keep.tile([P, PACK - split, P, PACK], BF16, name="q_high%d" % g, align_bytes=64)
+            if g == 0:
+                deal(nc.scalar.copy, low, q_first[:], 0, 0)
+                deal(nc.scalar.copy, high, q_first[:], 0, split)
+                deal(nc.vector.tensor_copy, low, q_second, 2, 0)
+                deal(nc.scalar.copy, high, q_second, 2, split)
+            else:
+                deal(nc.vector.tensor_copy, low, q_last, 0, 0)
+                deal(nc.scalar.copy, high, q_last, 0, split)
+            for u in range(PACK):
+                grouped = low[:, u] if u < split else high[:, u - split]
+                q_codes = keep.tile([P, P], U32, name="q_codes%d_%d" % (g, u), align_bytes=64)
+                q_scale = keep.tile([P, P], U8, name="q_scale%d_%d" % (g, u), align_bytes=64)
+                nc.vector.quantize_mx(out=q_codes[:].bitcast(FP8X4), scales=q_scale[:],
+                                      in_=grouped.rearrange("p m j -> p (m j)"))
+                nc.tensor.matmul_mx(out=scores[u][:], lhsT=q_codes[:].bitcast(FP8X4), lhsT_scale=q_scale[:],
+                                    rhs=k_codes[:].bitcast(FP4X4), rhs_scale=k_planes[:, g * N:(g + 1) * N],
+                                    start=(g == 0), stop=(g == PASSES - 1))
+
+        y_rows = out_0.rearrange("(p u) i -> p u i", u=PACK)
+        y = []
+        for h in range(2):
+            cols = slice(h * HALF, (h + 1) * HALF)
+            y_half = keep.tile([P, PACK, HALF], F32, name="y%d" % h)
+            for u in range(PACK):
+                z = keep.tile([P, HALF], F32, name="z%d_%d" % (h, u))
+                nc.vector.scalar_tensor_tensor(z[:], scores[u][:, cols], lse[:, u:u + 1], bias_all[:, cols],
+                                               ALU.subtract, ALU.add)
+                nc.scalar.activation(y_half[:, u, :], z[:], ACT.Exp)
+                if u % 2 == 1:
+                    nc.sync.dma_start(y_rows[:, u - 1:u + 1, cols], y_half[:, u - 1:u + 1, :])
+            y.append(y_half)
+
+        y_scale = keep.tile([P, N], U8, name="y_scale", align_bytes=64)
+        y_codes = keep.tile([P, N], I32, name="y_codes", align_bytes=64)
+        words_out = out_1[0].rearrange("p i b -> p (i b)").bitcast(I32)
+        for first, last, engine in ((0, 256, nc.vector.tensor_copy), (256, 384, nc.vector.tensor_copy), (384, 512, nc.scalar.copy)):
+            h = first // HALF
+            woven = keep.tile([P, last - first, PACK], BF16, name="woven%d" % first, align_bytes=64)
+            engine(woven[:].rearrange("p (c k) u -> p c u k", k=4),
+                   y[h][:, :, first - h * HALF:last - h * HALF].rearrange("p u (c k) -> p c u k", k=4))
+            nc.vector.quantize_mx(out=y_codes[:, first:last].bitcast(FP8X4), scales=y_scale[:, first:last],
+                                  in_=woven[:].rearrange("p i u -> p (i u)"))
+            if last % HALF == 0:
+                nc.sync.dma_start(words_out[:, last - HALF:last], y_codes[:, last - HALF:last])
+        scales_out = out_2[0].bitcast(I32)
+        for quad in range(4):
+            queue = nc.sync if quad < 2 else nc.scalar
+            queue.dma_start(scales_out[4 * quad:4 * quad + 4, :], y_scale[:].bitcast(I32)[32 * quad:32 * quad + 4, :])

@@ -40,6 +40,8 @@ def tile_attend_plq_recomp_topk_kernel(tc, qT, k_words, k_scales, kb, ls, offs, 
         nc.sync.dma_start(q_first[:], q_rows[0, :, 0:2, :])
         word_pool = keep.tile([P, T], I32, name="word_pool", align_bytes=64)
         nc.sync.dma_start(word_pool[:], k_words[0].rearrange("p t b -> p (t b)").bitcast(I32))
+        q_second = keep.tile([P, 2, NQ], F32, name="q_second")
+        nc.sync.dma_start(q_second[:], q_rows[0, :, 2:4, :])
 
         warm_in = keep.tile([P, 1], F32, name="warm_in")
         warm_out = keep.tile([P, 1], F32, name="warm_out")
@@ -52,21 +54,20 @@ def tile_attend_plq_recomp_topk_kernel(tc, qT, k_words, k_scales, kb, ls, offs, 
         nc.vector.memset(scale_words[0:96, :], 0)
 
         k_planes = keep.tile([P, PASSES * N], U8, name="k_planes", align_bytes=64)
-        nc.gpsimd.memset(k_planes[:].bitcast(I32), 0)
+        nc.vector.memset(k_planes[:].bitcast(I32), 0)
         ident = keep.tile([P, P], F32, name="ident")
-        make_identity(nc, ident[:])
+        nc.vector.memset(ident[:], 0.0)
+        make_identity(nc, ident[:], nomemset=True)
         lse = keep.tile([P, PACK], F32, name="lse")
         nc.gpsimd.dma_start(lse[:], ls[0].rearrange("(p u) o -> p (u o)", u=PACK))
 
         k_rows = keep.tile([P, N], U8, name="k_rows", align_bytes=64)
         nc.vector.tensor_copy(k_rows[:], scale_pool[:].indirect(offsets[:]))
-        q_rest = keep.tile([P, 6, NQ], F32, name="q_rest", tag="q_rest", align_bytes=64)
-        q_second, q_last = q_rest[:, 0:2, :], q_rest[:, 2:6, :]
-        nc.sync.dma_start(q_second, q_rows[0, :, 2:4, :])
+        q_last = keep.tile([P, PACK, NQ], F32, name="q_last", tag="q_rest", align_bytes=64)
         for quad in range(4):
-            nc.sync.dma_start(k_planes[:].bitcast(I32)[32 * quad:32 * quad + 4, :],
-                              k_rows[:].bitcast(I32)[96 + 8 * quad:96 + 8 * quad + 8, :])
-        nc.sync.dma_start(q_last, q_rows[1])
+            nc.scalar.dma_start(k_planes[:].bitcast(I32)[32 * quad:32 * quad + 4, :],
+                                k_rows[:].bitcast(I32)[96 + 8 * quad:96 + 8 * quad + 8, :])
+        nc.sync.dma_start(q_last[:], q_rows[1])
 
         bias_row = keep.tile([P, N], F32, name="bias_row", align_bytes=64)
         nc.vector.tensor_copy(bias_row[:], bias_pool[:].indirect(offsets[:]))
@@ -79,7 +80,7 @@ def tile_attend_plq_recomp_topk_kernel(tc, qT, k_words, k_scales, kb, ls, offs, 
         for s in range(N // P):
             nc.tensor.transpose(turned[:, s, :], bias_row[:, s * P:(s + 1) * P], ident[:])
         bias_cols = keep.tile([P, N // P], F32, name="bias_cols")
-        nc.scalar.copy(bias_cols[:], turned[:, :, 0])
+        nc.vector.tensor_copy(bias_cols[:], turned[:, :, 0])
         spread = psum.tile([P, N], F32, name="spread")
         for s in range(N // P):
             nc.tensor.transpose(spread[:, s * P:(s + 1) * P], bias_cols[:, s:s + 1].to_broadcast([P, P]), ident[:])
@@ -96,17 +97,17 @@ def tile_attend_plq_recomp_topk_kernel(tc, qT, k_words, k_scales, kb, ls, offs, 
         for g in range(PASSES):
             k_codes = keep.tile([P, N], U16, name="k_codes%d" % g, align_bytes=64)
             nc.vector.tensor_copy(k_codes[:], halves[:, g, :])
-            split = 2 if g == 0 else 3
+            split = 2
             low = keep.tile([P, split, P, PACK], BF16, name="q_low%d" % g, align_bytes=64)
             high = keep.tile([P, PACK - split, P, PACK], BF16, name="q_high%d" % g, align_bytes=64)
             if g == 0:
                 deal(nc.scalar.copy, low, q_first[:], 0, 0)
                 deal(nc.scalar.copy, high, q_first[:], 0, split)
-                deal(nc.vector.tensor_copy, low, q_second, 2, 0)
-                deal(nc.scalar.copy, high, q_second, 2, split)
+                deal(nc.scalar.copy, low, q_second[:], 2, 0)
+                deal(nc.scalar.copy, high, q_second[:], 2, split)
             else:
-                deal(nc.vector.tensor_copy, low, q_last, 0, 0)
-                deal(nc.scalar.copy, high, q_last, 0, split)
+                deal(nc.vector.tensor_copy, low, q_last[:], 0, 0)
+                deal(nc.scalar.copy, high, q_last[:], 0, split)
             for u in range(PACK):
                 grouped = low[:, u] if u < split else high[:, u - split]
                 q_codes = keep.tile([P, P], U32, name="q_codes%d_%d" % (g, u), align_bytes=64)
@@ -134,13 +135,17 @@ def tile_attend_plq_recomp_topk_kernel(tc, qT, k_words, k_scales, kb, ls, offs, 
         y_scale = keep.tile([P, N], U8, name="y_scale", align_bytes=64)
         y_codes = keep.tile([P, N], I32, name="y_codes", align_bytes=64)
         words_out = out_1[0].rearrange("p i b -> p (i b)").bitcast(I32)
-        for first, last, engine in ((0, 256, nc.vector.tensor_copy), (256, 384, nc.vector.tensor_copy), (384, 512, nc.scalar.copy)):
+        pieces = ((0, 256, nc.vector.tensor_copy), (256, 384, nc.vector.tensor_copy), (384, 512, nc.scalar.copy))
+        woven = []
+        for first, last, engine in pieces:
             h = first // HALF
-            woven = keep.tile([P, last - first, PACK], BF16, name="woven%d" % first, align_bytes=64)
-            engine(woven[:].rearrange("p (c k) u -> p c u k", k=4),
+            piece = keep.tile([P, last - first, PACK], BF16, name="woven%d" % first, align_bytes=64)
+            engine(piece[:].rearrange("p (c k) u -> p c u k", k=4),
                    y[h][:, :, first - h * HALF:last - h * HALF].rearrange("p u (c k) -> p c u k", k=4))
+            woven.append(piece)
+        for (first, last, engine), piece in zip(pieces, woven):
             nc.vector.quantize_mx(out=y_codes[:, first:last].bitcast(FP8X4), scales=y_scale[:, first:last],
-                                  in_=woven[:].rearrange("p i u -> p (i u)"))
+                                  in_=piece[:].rearrange("p i u -> p (i u)"))
             if last % HALF == 0:
                 nc.sync.dma_start(words_out[:, last - HALF:last], y_codes[:, last - HALF:last])
         scales_out = out_2[0].bitcast(I32)

@@ -21,58 +21,65 @@ PASSES = D // (P * PACK)
 FLOPS = 2 * NQ * N * D
 
 HALF = N // 2
+PAIR = 2
+ROW_AT = 4 * T
+SCALE_AT = 8 * T
 
 
 def tile_attend_plq_recomp_topk_kernel(tc, qT, k_words, k_scales, kb, ls, offs, out_0, out_1, out_2):
     nc = tc.nc
     with ExitStack() as ctx:
         keep = ctx.enter_context(tc.tile_pool(name="keep", bufs=1))
+        shared = ctx.enter_context(tc.tile_pool(name="shared", bufs=1))
         psum = ctx.enter_context(tc.psum_pool(name="psum", bufs=1))
 
         q_rows = qT[0].rearrange("(g p j) q -> g p j q", g=PASSES, j=PACK)
 
         offsets = keep.tile([P, N // 16], U16, name="offsets")
         nc.sync.dma_start(offsets[:], offs)
-        scale_pool = keep.tile([P, T], U8, name="scale_pool", tag="q_rest", align_bytes=64)
+        scale_pool = shared.tile([P, T], U8, name="scale_pool", offset=SCALE_AT, align_bytes=64)
         scale_words = scale_pool[:].bitcast(I32)
         nc.sync.dma_start(scale_words[96:128, :], k_scales.bitcast(I32).rearrange("o f t -> f o t"))
-        q_first = keep.tile([P, 2, NQ], F32, name="q_first")
-        nc.sync.dma_start(q_first[:], q_rows[0, :, 0:2, :])
+        kb_row = shared.tile([1, T], F32, name="kb_row", offset=ROW_AT, align_bytes=64)
+        nc.sync.dma_start(kb_row[:], kb[0:1, :])
+        q_first = keep.tile([P, PAIR, NQ], F32, name="q_first")
+        nc.sync.dma_start(q_first[:], q_rows[0, :, 0:PAIR, :])
         word_pool = keep.tile([P, T], I32, name="word_pool", align_bytes=64)
         nc.sync.dma_start(word_pool[:], k_words[0].rearrange("p t b -> p (t b)").bitcast(I32))
-        q_second = keep.tile([P, 2, NQ], F32, name="q_second")
-        nc.sync.dma_start(q_second[:], q_rows[0, :, 2:4, :])
+        lse = keep.tile([P, PACK], F32, name="lse")
+        nc.sync.dma_start(lse[:], ls[0].rearrange("(p u) o -> p (u o)", u=PACK))
 
         warm_in = keep.tile([P, 1], F32, name="warm_in")
         warm_out = keep.tile([P, 1], F32, name="warm_out")
         nc.gpsimd.memset(warm_in[:], 0.0)
         nc.scalar.activation(warm_out[:], warm_in[:], ACT.Exp)
 
-        bias_pool = keep.tile([P, T], F32, name="bias_pool", tag="bias_pool", align_bytes=64)
-        nc.vector.memset(bias_pool[:], 0.0)
-        nc.scalar.dma_start(bias_pool[0:1, :], kb[0:1, :])
         nc.vector.memset(scale_words[0:96, :], 0)
-
+        bias_pool = shared.tile([P, T], F32, name="bias_pool", offset=0, align_bytes=64)
+        nc.vector.memset(bias_pool[:], 0.0)
+        nc.scalar.copy(bias_pool[0:1, 0:T // 2], kb_row[:, 0:T // 2])
         k_planes = keep.tile([P, PASSES * N], U8, name="k_planes", align_bytes=64)
         nc.vector.memset(k_planes[:].bitcast(I32), 0)
         ident = keep.tile([P, P], F32, name="ident")
         nc.vector.memset(ident[:], 0.0)
         make_identity(nc, ident[:], nomemset=True)
-        lse = keep.tile([P, PACK], F32, name="lse")
-        nc.gpsimd.dma_start(lse[:], ls[0].rearrange("(p u) o -> p (u o)", u=PACK))
 
         k_rows = keep.tile([P, N], U8, name="k_rows", align_bytes=64)
         nc.vector.tensor_copy(k_rows[:], scale_pool[:].indirect(offsets[:]))
-        q_last = keep.tile([P, PACK, NQ], F32, name="q_last", tag="q_rest", align_bytes=64)
         for quad in range(4):
-            nc.scalar.dma_start(k_planes[:].bitcast(I32)[32 * quad:32 * quad + 4, :],
-                                k_rows[:].bitcast(I32)[96 + 8 * quad:96 + 8 * quad + 8, :])
-        nc.sync.dma_start(q_last[:], q_rows[1])
+            nc.sync.dma_start(k_planes[:].bitcast(I32)[32 * quad:32 * quad + 4, :],
+                              k_rows[:].bitcast(I32)[96 + 8 * quad:96 + 8 * quad + 8, :])
+        q_rest = shared.tile([P, 3, PAIR, NQ], F32, name="q_rest", offset=SCALE_AT, align_bytes=64)
+        q_raw = {(0, 0): q_first[:]}
+        for piece, (g, j0) in enumerate(((0, 2), (1, 0), (1, 2))):
+            nc.sync.dma_start(q_rest[:, piece], q_rows[g, :, j0:j0 + PAIR, :])
+            q_raw[g, j0] = q_rest[:, piece]
 
+        nc.vector.tensor_copy(bias_pool[0:1, T // 2:T], kb_row[:, T // 2:T])
         bias_row = keep.tile([P, N], F32, name="bias_row", align_bytes=64)
         nc.vector.tensor_copy(bias_row[:], bias_pool[:].indirect(offsets[:]))
 
-        k_pairs = keep.tile([P, N], U32, name="k_pairs", tag="bias_pool", align_bytes=64)
+        k_pairs = shared.tile([P, N], U32, name="k_pairs", offset=0, align_bytes=64)
         nc.vector.tensor_copy(k_pairs[:], word_pool[:].bitcast(U32).indirect(offsets[:]))
         halves = k_pairs[:].bitcast(U16).rearrange("p (i h) -> p h i", h=2)
 
@@ -80,7 +87,7 @@ def tile_attend_plq_recomp_topk_kernel(tc, qT, k_words, k_scales, kb, ls, offs, 
         for s in range(N // P):
             nc.tensor.transpose(turned[:, s, :], bias_row[:, s * P:(s + 1) * P], ident[:])
         bias_cols = keep.tile([P, N // P], F32, name="bias_cols")
-        nc.vector.tensor_copy(bias_cols[:], turned[:, :, 0])
+        nc.scalar.copy(bias_cols[:], turned[:, :, 0])
         spread = psum.tile([P, N], F32, name="spread")
         for s in range(N // P):
             nc.tensor.transpose(spread[:, s * P:(s + 1) * P], bias_cols[:, s:s + 1].to_broadcast([P, P]), ident[:])
@@ -88,28 +95,21 @@ def tile_attend_plq_recomp_topk_kernel(tc, qT, k_words, k_scales, kb, ls, offs, 
         nc.scalar.copy(bias_all[:], spread[:])
 
         def deal(engine, grouped, raw, j0, u0):
-            rows, count = raw.shape[1], grouped.shape[1]
-            src = raw.rearrange("p j (m u) -> p m j u", u=PACK)[:, :, :, u0:u0 + count]
-            dst = grouped[:].rearrange("p u m j -> p m j u")[:, :, j0:j0 + rows, :]
+            src = raw.rearrange("p j (m u) -> p m j u", u=PACK)[:, :, :, u0:u0 + PAIR]
+            dst = grouped[:].rearrange("p u m j -> p m j u")[:, :, j0:j0 + PAIR, :]
             engine(dst, src)
 
         scores = [psum.tile([P, N], F32, name="scores%d" % u) for u in range(PACK)]
         for g in range(PASSES):
             k_codes = keep.tile([P, N], U16, name="k_codes%d" % g, align_bytes=64)
             nc.vector.tensor_copy(k_codes[:], halves[:, g, :])
-            split = 2
-            low = keep.tile([P, split, P, PACK], BF16, name="q_low%d" % g, align_bytes=64)
-            high = keep.tile([P, PACK - split, P, PACK], BF16, name="q_high%d" % g, align_bytes=64)
-            if g == 0:
-                deal(nc.scalar.copy, low, q_first[:], 0, 0)
-                deal(nc.scalar.copy, high, q_first[:], 0, split)
-                deal(nc.scalar.copy, low, q_second[:], 2, 0)
-                deal(nc.scalar.copy, high, q_second[:], 2, split)
-            else:
-                deal(nc.vector.tensor_copy, low, q_last[:], 0, 0)
-                deal(nc.scalar.copy, high, q_last[:], 0, split)
+            low = keep.tile([P, PAIR, P, PACK], BF16, name="q_low%d" % g, align_bytes=64)
+            high = shared.tile([P, PAIR, P, PACK], BF16, name="q_high%d" % g, offset=ROW_AT + 2048 * g, align_bytes=64)
+            for j0 in (0, 2):
+                deal(nc.vector.tensor_copy, low, q_raw[g, j0], j0, 0)
+                deal(nc.scalar.copy, high, q_raw[g, j0], j0, PAIR)
             for u in range(PACK):
-                grouped = low[:, u] if u < split else high[:, u - split]
+                grouped = low[:, u] if u < PAIR else high[:, u - PAIR]
                 q_codes = keep.tile([P, P], U32, name="q_codes%d_%d" % (g, u), align_bytes=64)
                 q_scale = keep.tile([P, P], U8, name="q_scale%d_%d" % (g, u), align_bytes=64)
                 nc.vector.quantize_mx(out=q_codes[:].bitcast(FP8X4), scales=q_scale[:],

@@ -22,8 +22,14 @@ FLOPS = 2 * NQ * N * D
 
 HALF = N // 2
 PAIR = 2
-ROW_AT = 4 * T
-SCALE_AT = 8 * T
+ROW_SPLIT = 1344
+BIAS_AT = 0
+COLS_AT = 4 * T
+EARLY_AT = 5 * T
+SCALE_AT = 10 * T
+LOW_AT = 16 * T
+CODE_AT = 18 * T
+ROW_AT = 20 * T
 
 
 def tile_attend_plq_recomp_topk_kernel(tc, qT, k_words, k_scales, kb, ls, offs, out_0, out_1, out_2):
@@ -40,97 +46,109 @@ def tile_attend_plq_recomp_topk_kernel(tc, qT, k_words, k_scales, kb, ls, offs, 
         scale_pool = shared.tile([P, T], U8, name="scale_pool", offset=SCALE_AT, align_bytes=64)
         scale_words = scale_pool[:].bitcast(I32)
         nc.sync.dma_start(scale_words[96:128, :], k_scales.bitcast(I32).rearrange("o f t -> f o t"))
-        kb_row = shared.tile([1, T], F32, name="kb_row", offset=ROW_AT, align_bytes=64)
+        kb_row = keep.tile([1, T], F32, name="kb_row", align_bytes=64)
         nc.sync.dma_start(kb_row[:], kb[0:1, :])
-        q_first = keep.tile([P, PAIR, NQ], F32, name="q_first")
-        nc.sync.dma_start(q_first[:], q_rows[0, :, 0:PAIR, :])
         word_pool = keep.tile([P, T], I32, name="word_pool", align_bytes=64)
         nc.sync.dma_start(word_pool[:], k_words[0].rearrange("p t b -> p (t b)").bitcast(I32))
-        lse = keep.tile([P, PACK], F32, name="lse")
-        nc.sync.dma_start(lse[:], ls[0].rearrange("(p u) o -> p (u o)", u=PACK))
+        q_zero = shared.tile([P, PACK, NQ], F32, name="q_zero", offset=EARLY_AT, align_bytes=64)
+        for j0 in (0, 2):
+            nc.sync.dma_start(q_zero[:, j0:j0 + PAIR, :], q_rows[0, :, j0:j0 + PAIR, :])
 
+        nc.gpsimd.memset(scale_words[0:96, :], 0)
         warm_in = keep.tile([P, 1], F32, name="warm_in")
         warm_out = keep.tile([P, 1], F32, name="warm_out")
         nc.gpsimd.memset(warm_in[:], 0.0)
         nc.scalar.activation(warm_out[:], warm_in[:], ACT.Exp)
-
-        nc.vector.memset(scale_words[0:96, :], 0)
-        bias_pool = shared.tile([P, T], F32, name="bias_pool", offset=0, align_bytes=64)
-        nc.vector.memset(bias_pool[:], 0.0)
-        nc.scalar.copy(bias_pool[0:1, 0:T // 2], kb_row[:, 0:T // 2])
         k_planes = keep.tile([P, PASSES * N], U8, name="k_planes", align_bytes=64)
-        nc.vector.memset(k_planes[:].bitcast(I32), 0)
+        nc.gpsimd.memset(k_planes[:].bitcast(I32), 0)
         ident = keep.tile([P, P], F32, name="ident")
-        nc.vector.memset(ident[:], 0.0)
-        make_identity(nc, ident[:], nomemset=True)
+        make_identity(nc, ident[:])
+
+        bias_pool = shared.tile([P, T], F32, name="bias_pool", offset=BIAS_AT, align_bytes=64)
+        nc.vector.memset(bias_pool[:], 0.0)
+        nc.scalar.copy(bias_pool[0:1, 0:ROW_SPLIT], kb_row[:, 0:ROW_SPLIT])
 
         k_rows = keep.tile([P, N], U8, name="k_rows", align_bytes=64)
         nc.vector.tensor_copy(k_rows[:], scale_pool[:].indirect(offsets[:]))
         for quad in range(4):
             nc.sync.dma_start(k_planes[:].bitcast(I32)[32 * quad:32 * quad + 4, :],
                               k_rows[:].bitcast(I32)[96 + 8 * quad:96 + 8 * quad + 8, :])
-        q_rest = shared.tile([P, 3, PAIR, NQ], F32, name="q_rest", offset=SCALE_AT, align_bytes=64)
-        q_raw = {(0, 0): q_first[:]}
-        for piece, (g, j0) in enumerate(((0, 2), (1, 0), (1, 2))):
-            nc.sync.dma_start(q_rest[:, piece], q_rows[g, :, j0:j0 + PAIR, :])
-            q_raw[g, j0] = q_rest[:, piece]
+        q_one = shared.tile([P, PACK, NQ], F32, name="q_one", offset=SCALE_AT + 64, align_bytes=64)
+        nc.sync.dma_start(q_one[:], q_rows[1])
+        lse = shared.tile([P, PACK], F32, name="lse", offset=SCALE_AT, align_bytes=64)
+        nc.sync.dma_start(lse[:], ls[0].rearrange("(p u) o -> p (u o)", u=PACK))
 
-        nc.vector.tensor_copy(bias_pool[0:1, T // 2:T], kb_row[:, T // 2:T])
-        bias_row = keep.tile([P, N], F32, name="bias_row", align_bytes=64)
+        nc.vector.tensor_copy(bias_pool[0:1, ROW_SPLIT:T], kb_row[:, ROW_SPLIT:T])
+        bias_row = shared.tile([P, N], F32, name="bias_row", offset=ROW_AT, align_bytes=64)
         nc.vector.tensor_copy(bias_row[:], bias_pool[:].indirect(offsets[:]))
 
-        k_pairs = shared.tile([P, N], U32, name="k_pairs", offset=0, align_bytes=64)
+        k_pairs = shared.tile([P, N], U32, name="k_pairs", offset=BIAS_AT, align_bytes=64)
         nc.vector.tensor_copy(k_pairs[:], word_pool[:].bitcast(U32).indirect(offsets[:]))
         halves = k_pairs[:].bitcast(U16).rearrange("p (i h) -> p h i", h=2)
 
         turned = psum.tile([P, N // P, P], F32, name="turned")
         for s in range(N // P):
             nc.tensor.transpose(turned[:, s, :], bias_row[:, s * P:(s + 1) * P], ident[:])
-        bias_cols = keep.tile([P, N // P], F32, name="bias_cols")
+        bias_cols = shared.tile([P, N // P], F32, name="bias_cols", offset=COLS_AT, align_bytes=64)
         nc.scalar.copy(bias_cols[:], turned[:, :, 0])
         spread = psum.tile([P, N], F32, name="spread")
         for s in range(N // P):
             nc.tensor.transpose(spread[:, s * P:(s + 1) * P], bias_cols[:, s:s + 1].to_broadcast([P, P]), ident[:])
-        bias_all = keep.tile([P, N], F32, name="bias_all")
-        nc.scalar.copy(bias_all[:], spread[:])
 
-        def deal(engine, grouped, raw, j0, u0):
-            src = raw.rearrange("p j (m u) -> p m j u", u=PACK)[:, :, :, u0:u0 + PAIR]
-            dst = grouped[:].rearrange("p u m j -> p m j u")[:, :, j0:j0 + PAIR, :]
+        def deal(engine, grouped, raw, j0, j1, u0):
+            src = raw[:, j0:j1, :].rearrange("p j (m u) -> p m j u", u=PACK)[:, :, :, u0:u0 + PAIR]
+            dst = grouped[:].rearrange("p u m j -> p m j u")[:, :, j0:j1, :]
             engine(dst, src)
 
+        def part_words(g):
+            codes = keep.tile([P, N], U16, name="k_codes%d" % g, align_bytes=64)
+            nc.vector.tensor_copy(codes[:], halves[:, g, :])
+            return codes
+
         scores = [psum.tile([P, N], F32, name="scores%d" % u) for u in range(PACK)]
-        for g in range(PASSES):
-            k_codes = keep.tile([P, N], U16, name="k_codes%d" % g, align_bytes=64)
-            nc.vector.tensor_copy(k_codes[:], halves[:, g, :])
-            low = keep.tile([P, PAIR, P, PACK], BF16, name="q_low%d" % g, align_bytes=64)
-            high = shared.tile([P, PAIR, P, PACK], BF16, name="q_high%d" % g, offset=ROW_AT + 2048 * g, align_bytes=64)
-            for j0 in (0, 2):
-                deal(nc.vector.tensor_copy, low, q_raw[g, j0], j0, 0)
-                deal(nc.scalar.copy, high, q_raw[g, j0], j0, PAIR)
-            for u in range(PACK):
-                grouped = low[:, u] if u < PAIR else high[:, u - PAIR]
-                q_codes = keep.tile([P, P], U32, name="q_codes%d_%d" % (g, u), align_bytes=64)
-                q_scale = keep.tile([P, P], U8, name="q_scale%d_%d" % (g, u), align_bytes=64)
-                nc.vector.quantize_mx(out=q_codes[:].bitcast(FP8X4), scales=q_scale[:],
-                                      in_=grouped.rearrange("p m j -> p (m j)"))
-                nc.tensor.matmul_mx(out=scores[u][:], lhsT=q_codes[:].bitcast(FP8X4), lhsT_scale=q_scale[:],
-                                    rhs=k_codes[:].bitcast(FP4X4), rhs_scale=k_planes[:, g * N:(g + 1) * N],
-                                    start=(g == 0), stop=(g == PASSES - 1))
+
+        def multiply(g, u, grouped, k_codes, at):
+            q_codes = shared.tile([P, P], U32, name="q_codes%d_%d" % (g, u), offset=at, align_bytes=64)
+            q_scale = keep.tile([P, P], U8, name="q_scale%d_%d" % (g, u), align_bytes=64)
+            nc.vector.quantize_mx(out=q_codes[:].bitcast(FP8X4), scales=q_scale[:],
+                                  in_=grouped[:, u % PAIR].rearrange("p m j -> p (m j)"))
+            nc.tensor.matmul_mx(out=scores[u][:], lhsT=q_codes[:].bitcast(FP8X4), lhsT_scale=q_scale[:],
+                                rhs=k_codes[:].bitcast(FP4X4), rhs_scale=k_planes[:, g * N:(g + 1) * N],
+                                start=(g == 0), stop=(g == PASSES - 1))
+
+        low_zero = keep.tile([P, PAIR, P, PACK], BF16, name="low_zero", align_bytes=64)
+        high_zero = shared.tile([P, PAIR, P, PACK], BF16, name="high_zero", offset=ROW_AT, align_bytes=64)
+        low_one = shared.tile([P, PAIR, P, PACK], BF16, name="low_one", offset=LOW_AT, align_bytes=64)
+        high_one = keep.tile([P, PAIR, P, PACK], BF16, name="high_one", align_bytes=64)
+        codes_zero = part_words(0)
+        deal(nc.scalar.copy, low_zero, q_zero, 0, 2, 0)
+        deal(nc.vector.tensor_copy, low_zero, q_zero, 2, 4, 0)
+        deal(nc.scalar.copy, high_zero, q_zero, 0, 4, PAIR)
+        multiply(0, 0, low_zero, codes_zero, COLS_AT)
+        multiply(0, 1, low_zero, codes_zero, CODE_AT)
+        multiply(0, 2, high_zero, codes_zero, CODE_AT + 512)
+        codes_one = part_words(1)
+        bias_all = shared.tile([P, N], F32, name="bias_all", offset=EARLY_AT, align_bytes=64)
+        nc.scalar.copy(bias_all[:], spread[:])
+        deal(nc.vector.tensor_copy, low_one, q_one, 0, 4, 0)
+        deal(nc.scalar.copy, high_one, q_one, 0, 4, PAIR)
+        multiply(1, 0, low_one, codes_one, CODE_AT + 1024)
+        multiply(1, 1, low_one, codes_one, CODE_AT + 1536)
+        multiply(0, 3, high_zero, codes_zero, LOW_AT)
+        multiply(1, 2, high_one, codes_one, CODE_AT + 2048)
+        multiply(1, 3, high_one, codes_one, CODE_AT + 2560)
 
         y_rows = out_0.rearrange("(p u) i -> p u i", u=PACK)
-        y = []
-        for h in range(2):
-            cols = slice(h * HALF, (h + 1) * HALF)
-            y_half = keep.tile([P, PACK, HALF], F32, name="y%d" % h)
-            for u in range(PACK):
-                z = keep.tile([P, HALF], F32, name="z%d_%d" % (h, u))
-                nc.vector.scalar_tensor_tensor(z[:], scores[u][:, cols], lse[:, u:u + 1], bias_all[:, cols],
-                                               ALU.subtract, ALU.add)
-                nc.scalar.activation(y_half[:, u, :], z[:], ACT.Exp)
-                if u % 2 == 1:
-                    nc.sync.dma_start(y_rows[:, u - 1:u + 1, cols], y_half[:, u - 1:u + 1, :])
-            y.append(y_half)
+        y = keep.tile([P, PACK, N], F32, name="y")
+        steps = [(0, 0, N), (1, 0, N), (2, 0, N), (3, 0, HALF), (3, HALF, N)]
+        stores = {0: 0, 2: 1, 3: 3}
+        for u, first, last in steps:
+            z = keep.tile([P, last - first], F32, name="z%d_%d" % (u, first))
+            nc.vector.scalar_tensor_tensor(z[:], scores[u][:, first:last], lse[:, u:u + 1], bias_all[:, first:last],
+                                           ALU.subtract, ALU.add)
+            nc.scalar.activation(y[:, u, first:last], z[:], ACT.Exp)
+            if last == N and u in stores:
+                nc.sync.dma_start(y_rows[:, stores[u]:u + 1, :], y[:, stores[u]:u + 1, :])
 
         y_scale = keep.tile([P, N], U8, name="y_scale", align_bytes=64)
         y_codes = keep.tile([P, N], I32, name="y_codes", align_bytes=64)
@@ -138,10 +156,9 @@ def tile_attend_plq_recomp_topk_kernel(tc, qT, k_words, k_scales, kb, ls, offs, 
         pieces = ((0, 256, nc.vector.tensor_copy), (256, 384, nc.vector.tensor_copy), (384, 512, nc.scalar.copy))
         woven = []
         for first, last, engine in pieces:
-            h = first // HALF
             piece = keep.tile([P, last - first, PACK], BF16, name="woven%d" % first, align_bytes=64)
             engine(piece[:].rearrange("p (c k) u -> p c u k", k=4),
-                   y[h][:, :, first - h * HALF:last - h * HALF].rearrange("p u (c k) -> p c u k", k=4))
+                   y[:, :, first:last].rearrange("p u (c k) -> p c u k", k=4))
             woven.append(piece)
         for (first, last, engine), piece in zip(pieces, woven):
             nc.vector.quantize_mx(out=y_codes[:, first:last].bitcast(FP8X4), scales=y_scale[:, first:last],

@@ -22,14 +22,15 @@ FLOPS = 2 * NQ * N * D
 
 HALF = N // 2
 PAIR = 2
-ROW_SPLIT = 1344
+PIECE = PAIR * NQ * 4
 BIAS_AT = 0
-COLS_AT = 4 * T
-EARLY_AT = 5 * T
-SCALE_AT = 10 * T
-LOW_AT = 16 * T
-CODE_AT = 18 * T
-ROW_AT = 20 * T
+WORD_AT = BIAS_AT + 4 * T
+EARLY_AT = WORD_AT + 4 * T
+LATE_AT = EARLY_AT + 2 * PIECE
+SCALE_AT = LATE_AT + PIECE - T // 2
+LSE_AT = LATE_AT + PIECE
+STAGE_AT = LSE_AT + 2 * PIECE
+STAGE = PAIR * P * PACK * 2
 
 
 def tile_attend_plq_recomp_topk_kernel(tc, qT, k_words, k_scales, kb, ls, offs, out_0, out_1, out_2):
@@ -41,18 +42,21 @@ def tile_attend_plq_recomp_topk_kernel(tc, qT, k_words, k_scales, kb, ls, offs, 
 
         q_rows = qT[0].rearrange("(g p j) q -> g p j q", g=PASSES, j=PACK)
 
+        def load_q(g, j0, at):
+            raw = shared.tile([P, PAIR, NQ], F32, name="q_raw%d_%d" % (g, j0), offset=at, align_bytes=64)
+            nc.sync.dma_start(raw[:], q_rows[g, :, j0:j0 + PAIR, :])
+            return raw
+
         offsets = keep.tile([P, N // 16], U16, name="offsets")
         nc.sync.dma_start(offsets[:], offs)
         scale_pool = shared.tile([P, T], U8, name="scale_pool", offset=SCALE_AT, align_bytes=64)
         scale_words = scale_pool[:].bitcast(I32)
         nc.sync.dma_start(scale_words[96:128, :], k_scales.bitcast(I32).rearrange("o f t -> f o t"))
-        kb_row = keep.tile([1, T], F32, name="kb_row", align_bytes=64)
-        nc.sync.dma_start(kb_row[:], kb[0:1, :])
-        word_pool = keep.tile([P, T], I32, name="word_pool", align_bytes=64)
+        bias_pool = shared.tile([P, T], F32, name="bias_pool", offset=BIAS_AT, align_bytes=64)
+        nc.sync.dma_start(bias_pool[P - 1:P, :], kb[0:1, :])
+        word_pool = shared.tile([P, T], I32, name="word_pool", offset=WORD_AT, align_bytes=64)
         nc.sync.dma_start(word_pool[:], k_words[0].rearrange("p t b -> p (t b)").bitcast(I32))
-        q_zero = shared.tile([P, PACK, NQ], F32, name="q_zero", offset=EARLY_AT, align_bytes=64)
-        for j0 in (0, 2):
-            nc.sync.dma_start(q_zero[:, j0:j0 + PAIR, :], q_rows[0, :, j0:j0 + PAIR, :])
+        q_raw = {(0, 0): load_q(0, 0, EARLY_AT), (0, PAIR): load_q(0, PAIR, EARLY_AT + PIECE)}
 
         nc.gpsimd.memset(scale_words[0:96, :], 0)
         warm_in = keep.tile([P, 1], F32, name="warm_in")
@@ -63,25 +67,20 @@ def tile_attend_plq_recomp_topk_kernel(tc, qT, k_words, k_scales, kb, ls, offs, 
         nc.gpsimd.memset(k_planes[:].bitcast(I32), 0)
         ident = keep.tile([P, P], F32, name="ident")
         make_identity(nc, ident[:])
-
-        bias_pool = shared.tile([P, T], F32, name="bias_pool", offset=BIAS_AT, align_bytes=64)
-        nc.vector.memset(bias_pool[:], 0.0)
-        nc.scalar.copy(bias_pool[0:1, 0:ROW_SPLIT], kb_row[:, 0:ROW_SPLIT])
+        nc.vector.memset(bias_pool[0:P - 1, :], 0.0)
 
         k_rows = keep.tile([P, N], U8, name="k_rows", align_bytes=64)
         nc.vector.tensor_copy(k_rows[:], scale_pool[:].indirect(offsets[:]))
         for quad in range(4):
             nc.sync.dma_start(k_planes[:].bitcast(I32)[32 * quad:32 * quad + 4, :],
                               k_rows[:].bitcast(I32)[96 + 8 * quad:96 + 8 * quad + 8, :])
-        q_one = shared.tile([P, PACK, NQ], F32, name="q_one", offset=SCALE_AT + 64, align_bytes=64)
-        nc.sync.dma_start(q_one[:], q_rows[1])
-        lse = shared.tile([P, PACK], F32, name="lse", offset=SCALE_AT, align_bytes=64)
+        q_raw[1, 0] = load_q(1, 0, LATE_AT)
+        q_raw[1, PAIR] = load_q(1, PAIR, LSE_AT + 64)
+        lse = shared.tile([P, PACK], F32, name="lse", offset=LSE_AT, align_bytes=64)
         nc.sync.dma_start(lse[:], ls[0].rearrange("(p u) o -> p (u o)", u=PACK))
 
-        nc.vector.tensor_copy(bias_pool[0:1, ROW_SPLIT:T], kb_row[:, ROW_SPLIT:T])
-        bias_row = shared.tile([P, N], F32, name="bias_row", offset=ROW_AT, align_bytes=64)
+        bias_row = shared.tile([P, N], F32, name="bias_row", offset=STAGE_AT + STAGE, align_bytes=64)
         nc.vector.tensor_copy(bias_row[:], bias_pool[:].indirect(offsets[:]))
-
         k_pairs = shared.tile([P, N], U32, name="k_pairs", offset=BIAS_AT, align_bytes=64)
         nc.vector.tensor_copy(k_pairs[:], word_pool[:].bitcast(U32).indirect(offsets[:]))
         halves = k_pairs[:].bitcast(U16).rearrange("p (i h) -> p h i", h=2)
@@ -89,61 +88,45 @@ def tile_attend_plq_recomp_topk_kernel(tc, qT, k_words, k_scales, kb, ls, offs, 
         turned = psum.tile([P, N // P, P], F32, name="turned")
         for s in range(N // P):
             nc.tensor.transpose(turned[:, s, :], bias_row[:, s * P:(s + 1) * P], ident[:])
-        bias_cols = shared.tile([P, N // P], F32, name="bias_cols", offset=COLS_AT, align_bytes=64)
-        nc.scalar.copy(bias_cols[:], turned[:, :, 0])
+        bias_cols = keep.tile([P, N // P], F32, name="bias_cols", align_bytes=64)
+        nc.scalar.copy(bias_cols[:], turned[:, :, P - 1])
         spread = psum.tile([P, N], F32, name="spread")
         for s in range(N // P):
             nc.tensor.transpose(spread[:, s * P:(s + 1) * P], bias_cols[:, s:s + 1].to_broadcast([P, P]), ident[:])
+        bias_all = keep.tile([P, N], F32, name="bias_all", align_bytes=64)
+        nc.scalar.copy(bias_all[:], spread[:])
 
-        def deal(engine, grouped, raw, j0, j1, u0):
-            src = raw[:, j0:j1, :].rearrange("p j (m u) -> p m j u", u=PACK)[:, :, :, u0:u0 + PAIR]
-            dst = grouped[:].rearrange("p u m j -> p m j u")[:, :, j0:j1, :]
-            engine(dst, src)
-
-        def part_words(g):
+        k_codes = []
+        for g in range(PASSES):
             codes = keep.tile([P, N], U16, name="k_codes%d" % g, align_bytes=64)
             nc.vector.tensor_copy(codes[:], halves[:, g, :])
-            return codes
+            k_codes.append(codes)
 
         scores = [psum.tile([P, N], F32, name="scores%d" % u) for u in range(PACK)]
-
-        def multiply(g, u, grouped, k_codes, at):
-            q_codes = shared.tile([P, P], U32, name="q_codes%d_%d" % (g, u), offset=at, align_bytes=64)
-            q_scale = keep.tile([P, P], U8, name="q_scale%d_%d" % (g, u), align_bytes=64)
-            nc.vector.quantize_mx(out=q_codes[:].bitcast(FP8X4), scales=q_scale[:],
-                                  in_=grouped[:, u % PAIR].rearrange("p m j -> p (m j)"))
-            nc.tensor.matmul_mx(out=scores[u][:], lhsT=q_codes[:].bitcast(FP8X4), lhsT_scale=q_scale[:],
-                                rhs=k_codes[:].bitcast(FP4X4), rhs_scale=k_planes[:, g * N:(g + 1) * N],
-                                start=(g == 0), stop=(g == PASSES - 1))
-
-        low_zero = keep.tile([P, PAIR, P, PACK], BF16, name="low_zero", align_bytes=64)
-        high_zero = shared.tile([P, PAIR, P, PACK], BF16, name="high_zero", offset=ROW_AT, align_bytes=64)
-        low_one = shared.tile([P, PAIR, P, PACK], BF16, name="low_one", offset=LOW_AT, align_bytes=64)
-        high_one = keep.tile([P, PAIR, P, PACK], BF16, name="high_one", align_bytes=64)
-        codes_zero = part_words(0)
-        deal(nc.scalar.copy, low_zero, q_zero, 0, 2, 0)
-        deal(nc.vector.tensor_copy, low_zero, q_zero, 2, 4, 0)
-        deal(nc.scalar.copy, high_zero, q_zero, 0, 4, PAIR)
-        multiply(0, 0, low_zero, codes_zero, COLS_AT)
-        multiply(0, 1, low_zero, codes_zero, CODE_AT)
-        multiply(0, 2, high_zero, codes_zero, CODE_AT + 512)
-        codes_one = part_words(1)
-        bias_all = shared.tile([P, N], F32, name="bias_all", offset=EARLY_AT, align_bytes=64)
-        nc.scalar.copy(bias_all[:], spread[:])
-        deal(nc.vector.tensor_copy, low_one, q_one, 0, 4, 0)
-        deal(nc.scalar.copy, high_one, q_one, 0, 4, PAIR)
-        multiply(1, 0, low_one, codes_one, CODE_AT + 1024)
-        multiply(1, 1, low_one, codes_one, CODE_AT + 1536)
-        multiply(0, 3, high_zero, codes_zero, LOW_AT)
-        multiply(1, 2, high_one, codes_one, CODE_AT + 2048)
-        multiply(1, 3, high_one, codes_one, CODE_AT + 2560)
+        for g in range(PASSES):
+            grouped = [shared.tile([P, PAIR, P, PACK], BF16, name="grouped%d_%d" % (g, side), align_bytes=64,
+                                   offset=STAGE_AT + STAGE * ((g + side) % 2)) for side in range(2)]
+            for j0 in (0, PAIR):
+                by_group = q_raw[g, j0][:].rearrange("p j (m u) -> p m j u", u=PACK)
+                for side, engine in enumerate((nc.vector.tensor_copy, nc.scalar.copy)):
+                    engine(grouped[side][:].rearrange("p u m j -> p m j u")[:, :, j0:j0 + PAIR, :],
+                           by_group[:, :, :, side * PAIR:(side + 1) * PAIR])
+            for u in range(PACK):
+                q_codes = keep.tile([P, P], U32, name="q_codes%d_%d" % (g, u), align_bytes=64)
+                q_scale = keep.tile([P, P], U8, name="q_scale%d_%d" % (g, u), align_bytes=64)
+                nc.vector.quantize_mx(out=q_codes[:].bitcast(FP8X4), scales=q_scale[:],
+                                      in_=grouped[u // PAIR][:, u % PAIR].rearrange("p m j -> p (m j)"))
+                nc.tensor.matmul_mx(out=scores[u][:], lhsT=q_codes[:].bitcast(FP8X4), lhsT_scale=q_scale[:],
+                                    rhs=k_codes[g][:].bitcast(FP4X4), rhs_scale=k_planes[:, g * N:(g + 1) * N],
+                                    start=(g == 0), stop=(g == PASSES - 1))
 
         y_rows = out_0.rearrange("(p u) i -> p u i", u=PACK)
         y = keep.tile([P, PACK, N], F32, name="y")
         steps = [(0, 0, N), (1, 0, N), (2, 0, N), (3, 0, HALF), (3, HALF, N)]
         stores = {0: 0, 2: 1, 3: 3}
         for u, first, last in steps:
-            z = keep.tile([P, last - first], F32, name="z%d_%d" % (u, first))
+            z = shared.tile([P, last - first], F32, name="z%d_%d" % (u, first), align_bytes=64,
+                            offset=STAGE_AT + (u * N + first) * 4)
             nc.vector.scalar_tensor_tensor(z[:], scores[u][:, first:last], lse[:, u:u + 1], bias_all[:, first:last],
                                            ALU.subtract, ALU.add)
             nc.scalar.activation(y[:, u, first:last], z[:], ACT.Exp)

@@ -29,7 +29,8 @@ EARLY_AT = WORD_AT + 4 * T
 LATE_AT = EARLY_AT + 2 * PIECE
 SCALE_AT = LATE_AT + PIECE - T // 2
 LSE_AT = LATE_AT + PIECE
-STAGE_AT = LSE_AT + 2 * PIECE
+STAGE_AT = LSE_AT + 3 * PIECE
+CODES_AT = (WORD_AT, EARLY_AT + PIECE + 4 * N)
 STAGE = PAIR * P * PACK * 2
 
 
@@ -42,10 +43,10 @@ def tile_attend_plq_recomp_topk_kernel(tc, qT, k_words, k_scales, kb, ls, offs, 
 
         q_rows = qT[0].rearrange("(g p j) q -> g p j q", g=PASSES, j=PACK)
 
-        def load_q(g, j0, at):
-            raw = shared.tile([P, PAIR, NQ], F32, name="q_raw%d_%d" % (g, j0), offset=at, align_bytes=64)
-            nc.sync.dma_start(raw[:], q_rows[g, :, j0:j0 + PAIR, :])
-            return raw
+        def load_q(g, first, last, at):
+            raw = shared.tile([P, PACK, last - first], F32, name="q_raw%d_%d" % (g, first), offset=at, align_bytes=64)
+            nc.sync.dma_start(raw[:], q_rows[g, :, :, first:last])
+            return first, last, raw
 
         offsets = keep.tile([P, N // 16], U16, name="offsets")
         nc.sync.dma_start(offsets[:], offs)
@@ -56,7 +57,7 @@ def tile_attend_plq_recomp_topk_kernel(tc, qT, k_words, k_scales, kb, ls, offs, 
         nc.sync.dma_start(bias_pool[P - 1:P, :], kb[0:1, :])
         word_pool = shared.tile([P, T], I32, name="word_pool", offset=WORD_AT, align_bytes=64)
         nc.sync.dma_start(word_pool[:], k_words[0].rearrange("p t b -> p (t b)").bitcast(I32))
-        q_raw = {(0, 0): load_q(0, 0, EARLY_AT), (0, PAIR): load_q(0, PAIR, EARLY_AT + PIECE)}
+        q_raw = [[load_q(0, 0, NQ // 2, EARLY_AT), load_q(0, NQ // 2, NQ, EARLY_AT + PIECE)]]
 
         nc.gpsimd.memset(scale_words[0:96, :], 0)
         warm_in = keep.tile([P, 1], F32, name="warm_in")
@@ -74,8 +75,7 @@ def tile_attend_plq_recomp_topk_kernel(tc, qT, k_words, k_scales, kb, ls, offs, 
         for quad in range(4):
             nc.sync.dma_start(k_planes[:].bitcast(I32)[32 * quad:32 * quad + 4, :],
                               k_rows[:].bitcast(I32)[96 + 8 * quad:96 + 8 * quad + 8, :])
-        q_raw[1, 0] = load_q(1, 0, LATE_AT)
-        q_raw[1, PAIR] = load_q(1, PAIR, LSE_AT + 64)
+        q_raw.append([load_q(1, 0, NQ // 2, LATE_AT), load_q(1, NQ // 2, NQ, LSE_AT + 64)])
         lse = shared.tile([P, PACK], F32, name="lse", offset=LSE_AT, align_bytes=64)
         nc.sync.dma_start(lse[:], ls[0].rearrange("(p u) o -> p (u o)", u=PACK))
 
@@ -93,37 +93,35 @@ def tile_attend_plq_recomp_topk_kernel(tc, qT, k_words, k_scales, kb, ls, offs, 
         spread = psum.tile([P, N], F32, name="spread")
         for s in range(N // P):
             nc.tensor.transpose(spread[:, s * P:(s + 1) * P], bias_cols[:, s:s + 1].to_broadcast([P, P]), ident[:])
-        bias_all = keep.tile([P, N], F32, name="bias_all", align_bytes=64)
-        nc.scalar.copy(bias_all[:], spread[:])
-
-        k_codes = []
-        for g in range(PASSES):
-            codes = keep.tile([P, N], U16, name="k_codes%d" % g, align_bytes=64)
-            nc.vector.tensor_copy(codes[:], halves[:, g, :])
-            k_codes.append(codes)
+        bias_all = shared.tile([P, N], F32, name="bias_all", offset=EARLY_AT + PIECE, align_bytes=64)
 
         scores = [psum.tile([P, N], F32, name="scores%d" % u) for u in range(PACK)]
         for g in range(PASSES):
+            k_codes = shared.tile([P, N], U16, name="k_codes%d" % g, offset=CODES_AT[g], align_bytes=64)
+            nc.vector.tensor_copy(k_codes[:], halves[:, g, :])
             grouped = [shared.tile([P, PAIR, P, PACK], BF16, name="grouped%d_%d" % (g, side), align_bytes=64,
                                    offset=STAGE_AT + STAGE * ((g + side) % 2)) for side in range(2)]
-            for j0 in (0, PAIR):
-                by_group = q_raw[g, j0][:].rearrange("p j (m u) -> p m j u", u=PACK)
-                for side, engine in enumerate((nc.vector.tensor_copy, nc.scalar.copy)):
-                    engine(grouped[side][:].rearrange("p u m j -> p m j u")[:, :, j0:j0 + PAIR, :],
+            for first, last, raw in q_raw[g]:
+                by_group = raw[:].rearrange("p j (m u) -> p m j u", u=PACK)
+                low = nc.scalar.copy if (g, first) == (0, 0) else nc.vector.tensor_copy
+                for side, engine in enumerate((low, nc.scalar.copy)):
+                    engine(grouped[side][:].rearrange("p u m j -> p m j u")[:, first // PACK:last // PACK],
                            by_group[:, :, :, side * PAIR:(side + 1) * PAIR])
+            if g == 0:
+                nc.scalar.copy(bias_all[:], spread[:])
             for u in range(PACK):
                 q_codes = keep.tile([P, P], U32, name="q_codes%d_%d" % (g, u), align_bytes=64)
                 q_scale = keep.tile([P, P], U8, name="q_scale%d_%d" % (g, u), align_bytes=64)
                 nc.vector.quantize_mx(out=q_codes[:].bitcast(FP8X4), scales=q_scale[:],
                                       in_=grouped[u // PAIR][:, u % PAIR].rearrange("p m j -> p (m j)"))
                 nc.tensor.matmul_mx(out=scores[u][:], lhsT=q_codes[:].bitcast(FP8X4), lhsT_scale=q_scale[:],
-                                    rhs=k_codes[g][:].bitcast(FP4X4), rhs_scale=k_planes[:, g * N:(g + 1) * N],
+                                    rhs=k_codes[:].bitcast(FP4X4), rhs_scale=k_planes[:, g * N:(g + 1) * N],
                                     start=(g == 0), stop=(g == PASSES - 1))
 
         y_rows = out_0.rearrange("(p u) i -> p u i", u=PACK)
         y = keep.tile([P, PACK, N], F32, name="y")
-        steps = [(0, 0, N), (1, 0, N), (2, 0, N), (3, 0, HALF), (3, HALF, N)]
-        stores = {0: 0, 2: 1, 3: 3}
+        steps = [(0, 0, N), (1, 0, N), (2, 0, HALF), (3, 0, HALF), (2, HALF, N), (3, HALF, N)]
+        stores = {0: 0, 1: 1, 3: 2}
         for u, first, last in steps:
             z = shared.tile([P, last - first], F32, name="z%d_%d" % (u, first), align_bytes=64,
                             offset=STAGE_AT + (u * N + first) * 4)

@@ -30,7 +30,7 @@ LATE_AT = EARLY_AT + 2 * PIECE
 SCALE_AT = LATE_AT + PIECE - T // 2
 LSE_AT = LATE_AT + PIECE
 STAGE_AT = LSE_AT + 3 * PIECE
-CODES_AT = (WORD_AT, EARLY_AT + PIECE + 4 * N)
+CODES_AT = (WORD_AT, WORD_AT + 2 * N)
 STAGE = PAIR * P * PACK * 2
 
 
@@ -57,7 +57,7 @@ def tile_attend_plq_recomp_topk_kernel(tc, qT, k_words, k_scales, kb, ls, offs, 
         nc.sync.dma_start(bias_pool[P - 1:P, :], kb[0:1, :])
         word_pool = shared.tile([P, T], I32, name="word_pool", offset=WORD_AT, align_bytes=64)
         nc.sync.dma_start(word_pool[:], k_words[0].rearrange("p t b -> p (t b)").bitcast(I32))
-        q_raw = [[load_q(0, 0, NQ // 2, EARLY_AT), load_q(0, NQ // 2, NQ, EARLY_AT + PIECE)]]
+        q_raw = [[load_q(0, 0, NQ, EARLY_AT)]]
 
         nc.gpsimd.memset(scale_words[0:96, :], 0)
         warm_in = keep.tile([P, 1], F32, name="warm_in")
@@ -75,7 +75,7 @@ def tile_attend_plq_recomp_topk_kernel(tc, qT, k_words, k_scales, kb, ls, offs, 
         for quad in range(4):
             nc.sync.dma_start(k_planes[:].bitcast(I32)[32 * quad:32 * quad + 4, :],
                               k_rows[:].bitcast(I32)[96 + 8 * quad:96 + 8 * quad + 8, :])
-        q_raw.append([load_q(1, 0, NQ // 2, LATE_AT), load_q(1, NQ // 2, NQ, LSE_AT + 64)])
+        q_raw.append([load_q(1, 0, NQ, LSE_AT + 64)])
         lse = shared.tile([P, PACK], F32, name="lse", offset=LSE_AT, align_bytes=64)
         nc.sync.dma_start(lse[:], ls[0].rearrange("(p u) o -> p (u o)", u=PACK))
 
@@ -103,8 +103,7 @@ def tile_attend_plq_recomp_topk_kernel(tc, qT, k_words, k_scales, kb, ls, offs, 
                                    offset=STAGE_AT + STAGE * ((g + side) % 2)) for side in range(2)]
             for first, last, raw in q_raw[g]:
                 by_group = raw[:].rearrange("p j (m u) -> p m j u", u=PACK)
-                low = nc.scalar.copy if (g, first) == (0, 0) else nc.vector.tensor_copy
-                for side, engine in enumerate((low, nc.scalar.copy)):
+                for side, engine in enumerate((nc.vector.tensor_copy, nc.scalar.copy)):
                     engine(grouped[side][:].rearrange("p u m j -> p m j u")[:, first // PACK:last // PACK],
                            by_group[:, :, :, side * PAIR:(side + 1) * PAIR])
             if g == 0:
@@ -120,8 +119,8 @@ def tile_attend_plq_recomp_topk_kernel(tc, qT, k_words, k_scales, kb, ls, offs, 
 
         y_rows = out_0.rearrange("(p u) i -> p u i", u=PACK)
         y = keep.tile([P, PACK, N], F32, name="y")
-        steps = [(0, 0, N), (1, 0, N), (2, 0, HALF), (3, 0, HALF), (2, HALF, N), (3, HALF, N)]
-        stores = {0: 0, 1: 1, 3: 2}
+        steps = [(0, 0, HALF), (0, HALF, N), (1, 0, N), (2, 0, HALF), (3, 0, HALF), (2, HALF, N), (3, HALF, N)]
+        stores = {0: 0, 1: 1, 2: 2, 3: 3}
         for u, first, last in steps:
             z = shared.tile([P, last - first], F32, name="z%d_%d" % (u, first), align_bytes=64,
                             offset=STAGE_AT + (u * N + first) * 4)

@@ -22,6 +22,7 @@ FLOPS = 2 * NQ * N * D
 
 HALF = N // 2
 PAIR = 2
+SHARE = 84
 PIECE = PAIR * NQ * 4
 BIAS_AT = 0
 WORD_AT = BIAS_AT + 4 * T
@@ -103,9 +104,10 @@ def tile_attend_plq_recomp_topk_kernel(tc, qT, k_words, k_scales, kb, ls, offs, 
                                    offset=STAGE_AT + STAGE * ((g + side) % 2)) for side in range(2)]
             for first, last, raw in q_raw[g]:
                 by_group = raw[:].rearrange("p j (m u) -> p m j u", u=PACK)
-                for side, engine in enumerate((nc.vector.tensor_copy, nc.scalar.copy)):
-                    engine(grouped[side][:].rearrange("p u m j -> p m j u")[:, first // PACK:last // PACK],
-                           by_group[:, :, :, side * PAIR:(side + 1) * PAIR])
+                for side in range(2):
+                    for engine, m0, m1 in ((nc.vector.tensor_copy, 0, SHARE), (nc.scalar.copy, SHARE, P)):
+                        engine(grouped[side][:].rearrange("p u m j -> p m j u")[:, m0:m1],
+                               by_group[:, m0:m1, :, side * PAIR:(side + 1) * PAIR])
             if g == 0:
                 nc.scalar.copy(bias_all[:], spread[:])
             for u in range(PACK):

@@ -22,6 +22,7 @@ FLOPS = 2 * NQ * N * D
 
 HALF = N // 2
 PAIR = 2
+BANK = 2048
 SHARE = 84
 PIECE = PAIR * NQ * 4
 BIAS_AT = 0
@@ -53,7 +54,7 @@ def tile_attend_plq_recomp_topk_kernel(tc, qT, k_words, k_scales, kb, ls, offs, 
         nc.sync.dma_start(offsets[:], offs)
         scale_pool = shared.tile([P, T], U8, name="scale_pool", offset=SCALE_AT, align_bytes=64)
         scale_words = scale_pool[:].bitcast(I32)
-        nc.sync.dma_start(scale_words[96:128, :], k_scales.bitcast(I32).rearrange("o f t -> f o t"))
+        nc.sync.dma_start(scale_words[96:128, :], k_scales.bitcast(I32).rearrange("o f t -> (o f) t"))
         bias_pool = shared.tile([P, T], F32, name="bias_pool", offset=BIAS_AT, align_bytes=64)
         nc.sync.dma_start(bias_pool[P - 1:P, :], kb[0:1, :])
         word_pool = shared.tile([P, T], I32, name="word_pool", offset=WORD_AT, align_bytes=64)
@@ -73,10 +74,15 @@ def tile_attend_plq_recomp_topk_kernel(tc, qT, k_words, k_scales, kb, ls, offs, 
 
         k_rows = keep.tile([P, N], U8, name="k_rows", align_bytes=64)
         nc.vector.tensor_copy(k_rows[:], scale_pool[:].indirect(offsets[:]))
-        for quad in range(4):
-            nc.sync.dma_start(k_planes[:].bitcast(I32)[32 * quad:32 * quad + 4, :],
-                              k_rows[:].bitcast(I32)[96 + 8 * quad:96 + 8 * quad + 8, :])
+
+        def move_plane(g):
+            for r in range(4):
+                nc.sync.dma_start(k_planes[:, g * N:(g + 1) * N].bitcast(I32)[r:P:32, :],
+                                  k_rows[:].bitcast(I32)[96 + 16 * g + r:96 + 16 * (g + 1):4, :])
+
+        move_plane(0)
         q_raw.append([load_q(1, 0, NQ, LSE_AT + 64)])
+        move_plane(1)
         lse = shared.tile([P, PACK], F32, name="lse", offset=LSE_AT, align_bytes=64)
         nc.sync.dma_start(lse[:], ls[0].rearrange("(p u) o -> p (u o)", u=PACK))
 
@@ -86,17 +92,18 @@ def tile_attend_plq_recomp_topk_kernel(tc, qT, k_words, k_scales, kb, ls, offs, 
         nc.vector.tensor_copy(k_pairs[:], word_pool[:].bitcast(U32).indirect(offsets[:]))
         halves = k_pairs[:].bitcast(U16).rearrange("p (i h) -> p h i", h=2)
 
-        turned = psum.tile([P, N // P, P], F32, name="turned")
+        turned = psum.tile([P, N // P, P], F32, name="turned", offset=6 * BANK)
         for s in range(N // P):
             nc.tensor.transpose(turned[:, s, :], bias_row[:, s * P:(s + 1) * P], ident[:])
         bias_cols = keep.tile([P, N // P], F32, name="bias_cols", align_bytes=64)
         nc.scalar.copy(bias_cols[:], turned[:, :, P - 1])
-        spread = psum.tile([P, N], F32, name="spread")
+        spread = psum.tile([P, N], F32, name="spread", offset=7 * BANK)
         for s in range(N // P):
             nc.tensor.transpose(spread[:, s * P:(s + 1) * P], bias_cols[:, s:s + 1].to_broadcast([P, P]), ident[:])
         bias_all = shared.tile([P, N], F32, name="bias_all", offset=EARLY_AT + PIECE, align_bytes=64)
 
-        scores = [psum.tile([P, N], F32, name="scores%d" % u) for u in range(PACK)]
+        scores = [[psum.tile([P, HALF], F32, name="scores%d_%d" % (u, h), offset=(2 * u + h) * BANK)
+                   for h in range(2)] for u in range(PACK)]
         for g in range(PASSES):
             k_codes = shared.tile([P, N], U16, name="k_codes%d" % g, offset=CODES_AT[g], align_bytes=64)
             nc.vector.tensor_copy(k_codes[:], halves[:, g, :])
@@ -110,23 +117,32 @@ def tile_attend_plq_recomp_topk_kernel(tc, qT, k_words, k_scales, kb, ls, offs, 
                                by_group[:, m0:m1, :, side * PAIR:(side + 1) * PAIR])
             if g == 0:
                 nc.scalar.copy(bias_all[:], spread[:])
+            operands = []
             for u in range(PACK):
                 q_codes = keep.tile([P, P], U32, name="q_codes%d_%d" % (g, u), align_bytes=64)
                 q_scale = keep.tile([P, P], U8, name="q_scale%d_%d" % (g, u), align_bytes=64)
                 nc.vector.quantize_mx(out=q_codes[:].bitcast(FP8X4), scales=q_scale[:],
                                       in_=grouped[u // PAIR][:, u % PAIR].rearrange("p m j -> p (m j)"))
-                nc.tensor.matmul_mx(out=scores[u][:], lhsT=q_codes[:].bitcast(FP8X4), lhsT_scale=q_scale[:],
-                                    rhs=k_codes[:].bitcast(FP4X4), rhs_scale=k_planes[:, g * N:(g + 1) * N],
-                                    start=(g == 0), stop=(g == PASSES - 1))
+                operands.append((q_codes, q_scale))
+                if u % PAIR == PAIR - 1:
+                    for h in range(2):
+                        for v in range(u + 1 - PAIR, u + 1):
+                            for s in range(2):
+                                first = h * HALF + s * P
+                                nc.tensor.matmul_mx(
+                                    out=scores[v][h][:, s * P:(s + 1) * P], lhsT=operands[v][0][:].bitcast(FP8X4),
+                                    lhsT_scale=operands[v][1][:], rhs=k_codes[:, first:first + P].bitcast(FP4X4),
+                                    rhs_scale=k_planes[:, g * N + first:g * N + first + P],
+                                    start=(g == 0 and s == 0), stop=(g == PASSES - 1 and s == 1))
 
         y_rows = out_0.rearrange("(p u) i -> p u i", u=PACK)
         y = keep.tile([P, PACK, N], F32, name="y")
-        steps = [(0, 0, HALF), (0, HALF, N), (1, 0, N), (2, 0, HALF), (3, 0, HALF), (2, HALF, N), (3, HALF, N)]
+        steps = [(u, h * HALF, (h + 1) * HALF) for u0 in (0, PAIR) for h in range(2) for u in range(u0, u0 + PAIR)]
         stores = {0: 0, 1: 1, 2: 2, 3: 3}
         for u, first, last in steps:
             z = shared.tile([P, last - first], F32, name="z%d_%d" % (u, first), align_bytes=64,
                             offset=STAGE_AT + (u * N + first) * 4)
-            nc.vector.scalar_tensor_tensor(z[:], scores[u][:, first:last], lse[:, u:u + 1], bias_all[:, first:last],
+            nc.vector.scalar_tensor_tensor(z[:], scores[u][first // HALF][:], lse[:, u:u + 1], bias_all[:, first:last],
                                            ALU.subtract, ALU.add)
             nc.scalar.activation(y[:, u, first:last], z[:], ACT.Exp)
             if last == N and u in stores:

@@ -23,7 +23,10 @@ FLOPS = 2 * NQ * N * D
 HALF = N // 2
 PAIR = 2
 BANK = 2048
-SHARE = 84
+QUARTER = N // 4
+BANKS = (((0, 0, QUARTER),), ((0, QUARTER, HALF),), ((0, HALF, N),), ((1, 0, HALF),), ((1, HALF, N),),
+         ((2, 0, HALF),), ((3, 0, HALF),), ((2, HALF, N), (3, HALF, N)))
+SHARE = (84, 68)
 PIECE = PAIR * NQ * 4
 BIAS_AT = 0
 WORD_AT = BIAS_AT + 4 * T
@@ -102,8 +105,8 @@ def tile_attend_plq_recomp_topk_kernel(tc, qT, k_words, k_scales, kb, ls, offs, 
             nc.tensor.transpose(spread[:, s * P:(s + 1) * P], bias_cols[:, s:s + 1].to_broadcast([P, P]), ident[:])
         bias_all = shared.tile([P, N], F32, name="bias_all", offset=EARLY_AT + PIECE, align_bytes=64)
 
-        scores = [[psum.tile([P, HALF], F32, name="scores%d_%d" % (u, h), offset=(2 * u + h) * BANK)
-                   for h in range(2)] for u in range(PACK)]
+        banks = [psum.tile([P, len(held), held[0][2] - held[0][1]], F32, name="scores%d" % b, offset=b * BANK)
+                 for b, held in enumerate(BANKS)]
         for g in range(PASSES):
             k_codes = shared.tile([P, N], U16, name="k_codes%d" % g, offset=CODES_AT[g], align_bytes=64)
             nc.vector.tensor_copy(k_codes[:], halves[:, g, :])
@@ -112,7 +115,7 @@ def tile_attend_plq_recomp_topk_kernel(tc, qT, k_words, k_scales, kb, ls, offs, 
             for first, last, raw in q_raw[g]:
                 by_group = raw[:].rearrange("p j (m u) -> p m j u", u=PACK)
                 for side in range(2):
-                    for engine, m0, m1 in ((nc.vector.tensor_copy, 0, SHARE), (nc.scalar.copy, SHARE, P)):
+                    for engine, m0, m1 in ((nc.vector.tensor_copy, 0, SHARE[side]), (nc.scalar.copy, SHARE[side], P)):
                         engine(grouped[side][:].rearrange("p u m j -> p m j u")[:, m0:m1],
                                by_group[:, m0:m1, :, side * PAIR:(side + 1) * PAIR])
             if g == 0:
@@ -124,25 +127,25 @@ def tile_attend_plq_recomp_topk_kernel(tc, qT, k_words, k_scales, kb, ls, offs, 
                 nc.vector.quantize_mx(out=q_codes[:].bitcast(FP8X4), scales=q_scale[:],
                                       in_=grouped[u // PAIR][:, u % PAIR].rearrange("p m j -> p (m j)"))
                 operands.append((q_codes, q_scale))
-                if u % PAIR == PAIR - 1:
-                    for h in range(2):
-                        for v in range(u + 1 - PAIR, u + 1):
-                            for s in range(2):
-                                first = h * HALF + s * P
-                                nc.tensor.matmul_mx(
-                                    out=scores[v][h][:, s * P:(s + 1) * P], lhsT=operands[v][0][:].bitcast(FP8X4),
-                                    lhsT_scale=operands[v][1][:], rhs=k_codes[:, first:first + P].bitcast(FP4X4),
-                                    rhs_scale=k_planes[:, g * N + first:g * N + first + P],
-                                    start=(g == 0 and s == 0), stop=(g == PASSES - 1 and s == 1))
+            for bank, held in zip(banks, BANKS):
+                sums = [(place, u, first, at) for place, (u, first, last) in enumerate(held)
+                        for at in range(first, last, P)]
+                for n, (place, u, first, at) in enumerate(sums):
+                    nc.tensor.matmul_mx(
+                        out=bank[:, place, at - first:at - first + P], lhsT=operands[u][0][:].bitcast(FP8X4),
+                        lhsT_scale=operands[u][1][:], rhs=k_codes[:, at:at + P].bitcast(FP4X4),
+                        rhs_scale=k_planes[:, g * N + at:g * N + at + P],
+                        start=(g == 0 and n == 0), stop=(g == PASSES - 1 and n == len(sums) - 1))
 
         y_rows = out_0.rearrange("(p u) i -> p u i", u=PACK)
         y = keep.tile([P, PACK, N], F32, name="y")
-        steps = [(u, h * HALF, (h + 1) * HALF) for u0 in (0, PAIR) for h in range(2) for u in range(u0, u0 + PAIR)]
+        steps = [(bank[:, place, :], u, first, last) for bank, held in zip(banks, BANKS)
+                 for place, (u, first, last) in enumerate(held)]
         stores = {0: 0, 1: 1, 2: 2, 3: 3}
-        for u, first, last in steps:
+        for scores, u, first, last in steps:
             z = shared.tile([P, last - first], F32, name="z%d_%d" % (u, first), align_bytes=64,
                             offset=STAGE_AT + (u * N + first) * 4)
-            nc.vector.scalar_tensor_tensor(z[:], scores[u][first // HALF][:], lse[:, u:u + 1], bias_all[:, first:last],
+            nc.vector.scalar_tensor_tensor(z[:], scores, lse[:, u:u + 1], bias_all[:, first:last],
                                            ALU.subtract, ALU.add)
             nc.scalar.activation(y[:, u, first:last], z[:], ACT.Exp)
             if last == N and u in stores:

@@ -26,7 +26,7 @@ BANK = 2048
 QUARTER = N // 4
 BANKS = (((0, 0, QUARTER),), ((0, QUARTER, HALF),), ((0, HALF, N),), ((1, 0, HALF),), ((1, HALF, N),),
          ((2, 0, HALF),), ((3, 0, HALF),), ((2, HALF, N), (3, HALF, N)))
-SHARE = (84, 68)
+SHARE = ((84, 52), (84, 68))
 PIECE = PAIR * NQ * 4
 BIAS_AT = 0
 WORD_AT = BIAS_AT + 4 * T
@@ -35,8 +35,10 @@ LATE_AT = EARLY_AT + 2 * PIECE
 SCALE_AT = LATE_AT + PIECE - T // 2
 LSE_AT = LATE_AT + PIECE
 STAGE_AT = LSE_AT + 3 * PIECE
-CODES_AT = (WORD_AT, WORD_AT + 2 * N)
 STAGE = PAIR * P * PACK * 2
+GROUPED_AT = ((STAGE_AT, STAGE_AT + 3 * STAGE // 2), (STAGE_AT + STAGE, STAGE_AT + 2 * STAGE))
+CODES_AT = (WORD_AT, STAGE_AT)
+SUM_AT = GROUPED_AT[1][1]
 
 
 def tile_attend_plq_recomp_topk_kernel(tc, qT, k_words, k_scales, kb, ls, offs, out_0, out_1, out_2):
@@ -89,7 +91,7 @@ def tile_attend_plq_recomp_topk_kernel(tc, qT, k_words, k_scales, kb, ls, offs, 
         lse = shared.tile([P, PACK], F32, name="lse", offset=LSE_AT, align_bytes=64)
         nc.sync.dma_start(lse[:], ls[0].rearrange("(p u) o -> p (u o)", u=PACK))
 
-        bias_row = shared.tile([P, N], F32, name="bias_row", offset=STAGE_AT + STAGE, align_bytes=64)
+        bias_row = shared.tile([P, N], F32, name="bias_row", offset=GROUPED_AT[0][1], align_bytes=64)
         nc.vector.tensor_copy(bias_row[:], bias_pool[:].indirect(offsets[:]))
         k_pairs = shared.tile([P, N], U32, name="k_pairs", offset=BIAS_AT, align_bytes=64)
         nc.vector.tensor_copy(k_pairs[:], word_pool[:].bitcast(U32).indirect(offsets[:]))
@@ -111,11 +113,11 @@ def tile_attend_plq_recomp_topk_kernel(tc, qT, k_words, k_scales, kb, ls, offs, 
             k_codes = shared.tile([P, N], U16, name="k_codes%d" % g, offset=CODES_AT[g], align_bytes=64)
             nc.vector.tensor_copy(k_codes[:], halves[:, g, :])
             grouped = [shared.tile([P, PAIR, P, PACK], BF16, name="grouped%d_%d" % (g, side), align_bytes=64,
-                                   offset=STAGE_AT + STAGE * ((g + side) % 2)) for side in range(2)]
+                                   offset=GROUPED_AT[g][side]) for side in range(2)]
             for first, last, raw in q_raw[g]:
                 by_group = raw[:].rearrange("p j (m u) -> p m j u", u=PACK)
                 for side in range(2):
-                    for engine, m0, m1 in ((nc.vector.tensor_copy, 0, SHARE[side]), (nc.scalar.copy, SHARE[side], P)):
+                    for engine, m0, m1 in ((nc.vector.tensor_copy, 0, SHARE[g][side]), (nc.scalar.copy, SHARE[g][side], P)):
                         engine(grouped[side][:].rearrange("p u m j -> p m j u")[:, m0:m1],
                                by_group[:, m0:m1, :, side * PAIR:(side + 1) * PAIR])
             if g == 0:
@@ -144,7 +146,7 @@ def tile_attend_plq_recomp_topk_kernel(tc, qT, k_words, k_scales, kb, ls, offs, 
         stores = {0: 0, 1: 1, 2: 2, 3: 3}
         for scores, u, first, last in steps:
             z = shared.tile([P, last - first], F32, name="z%d_%d" % (u, first), align_bytes=64,
-                            offset=STAGE_AT + (u * N + first) * 4)
+                            offset=SUM_AT + (u * N + first) * 4)
             nc.vector.scalar_tensor_tensor(z[:], scores, lse[:, u:u + 1], bias_all[:, first:last],
                                            ALU.subtract, ALU.add)
             nc.scalar.activation(y[:, u, first:last], z[:], ACT.Exp)

@@ -26,18 +26,15 @@ BANK = 2048
 QUARTER = N // 4
 BANKS = (((0, 0, QUARTER),), ((0, QUARTER, HALF),), ((0, HALF, N),), ((1, 0, HALF),), ((1, HALF, N),),
          ((2, 0, HALF),), ((3, 0, HALF),), ((2, HALF, N), (3, HALF, N)))
-SHARE = ((84, 52), (84, 68))
-PIECE = PAIR * NQ * 4
-BIAS_AT = 0
-WORD_AT = BIAS_AT + 4 * T
-EARLY_AT = WORD_AT + 4 * T
-LATE_AT = EARLY_AT + 2 * PIECE
-SCALE_AT = LATE_AT + PIECE - T // 2
-LSE_AT = LATE_AT + PIECE
-STAGE_AT = LSE_AT + 3 * PIECE
+PIECES = ((0, 0, 128, 84, 76), (1, 0, 128, 84, 68))
+RAW = PACK * NQ * 4
 STAGE = PAIR * P * PACK * 2
-GROUPED_AT = ((STAGE_AT, STAGE_AT + 3 * STAGE // 2), (STAGE_AT + STAGE, STAGE_AT + 2 * STAGE))
-CODES_AT = (WORD_AT, STAGE_AT)
+RAW_AT = (0, RAW + T // 2 + 64)
+LSE_AT = RAW + T // 2
+SCALE_AT = LSE_AT - T // 2
+STAGE_AT = 3 * RAW
+GROUPED_AT = ((STAGE_AT, STAGE_AT + STAGE), (STAGE_AT + 2 * STAGE, STAGE_AT + 3 * STAGE))
+CODES_AT = (STAGE_AT - 1024, STAGE_AT - 2048)
 SUM_AT = GROUPED_AT[1][1]
 
 
@@ -50,21 +47,23 @@ def tile_attend_plq_recomp_topk_kernel(tc, qT, k_words, k_scales, kb, ls, offs, 
 
         q_rows = qT[0].rearrange("(g p j) q -> g p j q", g=PASSES, j=PACK)
 
-        def load_q(g, first, last, at):
-            raw = shared.tile([P, PACK, last - first], F32, name="q_raw%d_%d" % (g, first), offset=at, align_bytes=64)
-            nc.sync.dma_start(raw[:], q_rows[g, :, :, first:last])
-            return first, last, raw
+        def load_q(piece):
+            g, m0, m1 = PIECES[piece][:3]
+            raw = shared.tile([P, PACK, PACK * (m1 - m0)], F32, name="q_raw%d" % piece, offset=RAW_AT[piece],
+                              align_bytes=64)
+            nc.sync.dma_start(raw[:], q_rows[g, :, :, PACK * m0:PACK * m1])
+            return raw
 
         offsets = keep.tile([P, N // 16], U16, name="offsets")
         nc.sync.dma_start(offsets[:], offs)
         scale_pool = shared.tile([P, T], U8, name="scale_pool", offset=SCALE_AT, align_bytes=64)
         scale_words = scale_pool[:].bitcast(I32)
         nc.sync.dma_start(scale_words[96:128, :], k_scales.bitcast(I32).rearrange("o f t -> (o f) t"))
-        bias_pool = shared.tile([P, T], F32, name="bias_pool", offset=BIAS_AT, align_bytes=64)
+        bias_pool = keep.tile([P, T], F32, name="bias_pool", align_bytes=64)
         nc.sync.dma_start(bias_pool[P - 1:P, :], kb[0:1, :])
-        word_pool = shared.tile([P, T], I32, name="word_pool", offset=WORD_AT, align_bytes=64)
+        word_pool = keep.tile([P, T], I32, name="word_pool", align_bytes=64)
         nc.sync.dma_start(word_pool[:], k_words[0].rearrange("p t b -> p (t b)").bitcast(I32))
-        q_raw = [[load_q(0, 0, NQ, EARLY_AT)]]
+        q_raw = [load_q(0)]
 
         nc.gpsimd.memset(scale_words[0:96, :], 0)
         warm_in = keep.tile([P, 1], F32, name="warm_in")
@@ -86,14 +85,14 @@ def tile_attend_plq_recomp_topk_kernel(tc, qT, k_words, k_scales, kb, ls, offs, 
                                   k_rows[:].bitcast(I32)[96 + 16 * g + r:96 + 16 * (g + 1):4, :])
 
         move_plane(0)
-        q_raw.append([load_q(1, 0, NQ, LSE_AT + 64)])
+        q_raw.append(load_q(1))
         move_plane(1)
         lse = shared.tile([P, PACK], F32, name="lse", offset=LSE_AT, align_bytes=64)
         nc.sync.dma_start(lse[:], ls[0].rearrange("(p u) o -> p (u o)", u=PACK))
 
-        bias_row = shared.tile([P, N], F32, name="bias_row", offset=GROUPED_AT[0][1], align_bytes=64)
-        nc.vector.tensor_copy(bias_row[:], bias_pool[:].indirect(offsets[:]))
-        k_pairs = shared.tile([P, N], U32, name="k_pairs", offset=BIAS_AT, align_bytes=64)
+        bias_row = keep.tile([P, N], F32, name="bias_row", align_bytes=64)
+        nc.scalar.activation(bias_row[:], bias_pool[:].indirect(offsets[:]), ACT.Copy)
+        k_pairs = keep.tile([P, N], U32, name="k_pairs", align_bytes=64)
         nc.vector.tensor_copy(k_pairs[:], word_pool[:].bitcast(U32).indirect(offsets[:]))
         halves = k_pairs[:].bitcast(U16).rearrange("p (i h) -> p h i", h=2)
 
@@ -105,53 +104,70 @@ def tile_attend_plq_recomp_topk_kernel(tc, qT, k_words, k_scales, kb, ls, offs, 
         spread = psum.tile([P, N], F32, name="spread", offset=7 * BANK)
         for s in range(N // P):
             nc.tensor.transpose(spread[:, s * P:(s + 1) * P], bias_cols[:, s:s + 1].to_broadcast([P, P]), ident[:])
-        bias_all = shared.tile([P, N], F32, name="bias_all", offset=EARLY_AT + PIECE, align_bytes=64)
+        bias_all = keep.tile([P, N], F32, name="bias_all", align_bytes=64)
+        nc.scalar.copy(bias_all[:], spread[:])
 
         banks = [psum.tile([P, len(held), held[0][2] - held[0][1]], F32, name="scores%d" % b, offset=b * BANK)
                  for b, held in enumerate(BANKS)]
-        for g in range(PASSES):
+        q_codes = [[keep.tile([P, PAIR * P], U32, name="q_codes%d_%d" % (g, side), align_bytes=64)
+                    for side in range(2)] for g in range(PASSES)]
+        q_scale = [[keep.tile([P, PAIR * P], U8, name="q_scale%d_%d" % (g, side), align_bytes=64)
+                    for side in range(2)] for g in range(PASSES)]
+
+        def quantise(piece):
+            g, m0, m1 = PIECES[piece][:3]
+            grouped = [shared.tile([P, PAIR, m1 - m0, PACK], BF16, name="grouped%d_%d" % (piece, side),
+                                   align_bytes=64, offset=GROUPED_AT[piece][side]) for side in range(2)]
+            by_group = q_raw[piece][:].rearrange("p j (m u) -> p m j u", u=PACK)
+            for side in range(2):
+                share = PIECES[piece][3 + side]
+                for engine, a, b in ((nc.vector.tensor_copy, 0, share), (nc.scalar.copy, share, m1 - m0)):
+                    if a < b:
+                        engine(grouped[side][:].rearrange("p u m j -> p m j u")[:, a:b],
+                               by_group[:, a:b, :, side * PAIR:(side + 1) * PAIR])
+            for side, a, b in ((0, 0, 1), (0, 1, 2), (1, 0, 2)):
+                nc.vector.quantize_mx(out=q_codes[g][side][:, a * P:b * P].bitcast(FP8X4),
+                                      scales=q_scale[g][side][:, a * P:b * P],
+                                      in_=grouped[side][:, a:b].rearrange("p u m j -> p (u m j)"))
+
+        def part(g):
             k_codes = shared.tile([P, N], U16, name="k_codes%d" % g, offset=CODES_AT[g], align_bytes=64)
             nc.vector.tensor_copy(k_codes[:], halves[:, g, :])
-            grouped = [shared.tile([P, PAIR, P, PACK], BF16, name="grouped%d_%d" % (g, side), align_bytes=64,
-                                   offset=GROUPED_AT[g][side]) for side in range(2)]
-            for first, last, raw in q_raw[g]:
-                by_group = raw[:].rearrange("p j (m u) -> p m j u", u=PACK)
-                for side in range(2):
-                    for engine, m0, m1 in ((nc.vector.tensor_copy, 0, SHARE[g][side]), (nc.scalar.copy, SHARE[g][side], P)):
-                        engine(grouped[side][:].rearrange("p u m j -> p m j u")[:, m0:m1],
-                               by_group[:, m0:m1, :, side * PAIR:(side + 1) * PAIR])
-            if g == 0:
-                nc.scalar.copy(bias_all[:], spread[:])
-            operands = []
-            for u in range(PACK):
-                q_codes = keep.tile([P, P], U32, name="q_codes%d_%d" % (g, u), align_bytes=64)
-                q_scale = keep.tile([P, P], U8, name="q_scale%d_%d" % (g, u), align_bytes=64)
-                nc.vector.quantize_mx(out=q_codes[:].bitcast(FP8X4), scales=q_scale[:],
-                                      in_=grouped[u // PAIR][:, u % PAIR].rearrange("p m j -> p (m j)"))
-                operands.append((q_codes, q_scale))
+            return k_codes
+
+        def multiply(g, k_codes):
             for bank, held in zip(banks, BANKS):
+                width = P if g else held[0][2] - held[0][1]
                 sums = [(place, u, first, at) for place, (u, first, last) in enumerate(held)
-                        for at in range(first, last, P)]
+                        for at in range(first, last, width)]
                 for n, (place, u, first, at) in enumerate(sums):
                     nc.tensor.matmul_mx(
-                        out=bank[:, place, at - first:at - first + P], lhsT=operands[u][0][:].bitcast(FP8X4),
-                        lhsT_scale=operands[u][1][:], rhs=k_codes[:, at:at + P].bitcast(FP4X4),
-                        rhs_scale=k_planes[:, g * N + at:g * N + at + P],
+                        out=bank[:, place, at - first:at - first + width],
+                        lhsT=q_codes[g][u // PAIR][:, u % PAIR * P:(u % PAIR + 1) * P].bitcast(FP8X4),
+                        lhsT_scale=q_scale[g][u // PAIR][:, u % PAIR * P:(u % PAIR + 1) * P],
+                        rhs=k_codes[:, at:at + width].bitcast(FP4X4),
+                        rhs_scale=k_planes[:, g * N + at:g * N + at + width],
                         start=(g == 0 and n == 0), stop=(g == PASSES - 1 and n == len(sums) - 1))
+
+        codes0 = part(0)
+        codes1 = part(1)
+        quantise(0)
+        multiply(0, codes0)
+        quantise(1)
+        multiply(1, codes1)
 
         y_rows = out_0.rearrange("(p u) i -> p u i", u=PACK)
         y = keep.tile([P, PACK, N], F32, name="y")
         steps = [(bank[:, place, :], u, first, last) for bank, held in zip(banks, BANKS)
                  for place, (u, first, last) in enumerate(held)]
-        stores = {0: 0, 1: 1, 2: 2, 3: 3}
         for scores, u, first, last in steps:
             z = shared.tile([P, last - first], F32, name="z%d_%d" % (u, first), align_bytes=64,
                             offset=SUM_AT + (u * N + first) * 4)
             nc.vector.scalar_tensor_tensor(z[:], scores, lse[:, u:u + 1], bias_all[:, first:last],
                                            ALU.subtract, ALU.add)
             nc.scalar.activation(y[:, u, first:last], z[:], ACT.Exp)
-            if last == N and u in stores:
-                nc.sync.dma_start(y_rows[:, stores[u]:u + 1, :], y[:, stores[u]:u + 1, :])
+            if last == N:
+                nc.sync.dma_start(y_rows[:, u:u + 1, :], y[:, u:u + 1, :])
 
         y_scale = keep.tile([P, N], U8, name="y_scale", align_bytes=64)
         y_codes = keep.tile([P, N], I32, name="y_codes", align_bytes=64)

@@ -24,8 +24,7 @@ HALF = N // 2
 PAIR = 2
 BANK = 2048
 QUARTER = N // 4
-BANKS = (((0, 0, QUARTER),), ((0, QUARTER, HALF),), ((0, HALF, N),), ((1, 0, HALF),), ((1, HALF, N),),
-         ((2, 0, HALF),), ((3, 0, HALF),), ((2, HALF, N), (3, HALF, N)))
+BANKS = ((0, 0), (0, HALF), (1, 0), (1, HALF), (2, 0), (3, 0), (2, HALF), (3, HALF))
 PIECES = ((0, 0, 128, 84, 76), (1, 0, 128, 84, 68))
 RAW = PACK * NQ * 4
 STAGE = PAIR * P * PACK * 2
@@ -107,8 +106,7 @@ def tile_attend_plq_recomp_topk_kernel(tc, qT, k_words, k_scales, kb, ls, offs, 
         bias_all = keep.tile([P, N], F32, name="bias_all", align_bytes=64)
         nc.scalar.copy(bias_all[:], spread[:])
 
-        banks = [psum.tile([P, len(held), held[0][2] - held[0][1]], F32, name="scores%d" % b, offset=b * BANK)
-                 for b, held in enumerate(BANKS)]
+        banks = [psum.tile([P, HALF], F32, name="scores%d" % b, offset=b * BANK) for b in range(len(BANKS))]
         q_codes = [[keep.tile([P, PAIR * P], U32, name="q_codes%d_%d" % (g, side), align_bytes=64)
                     for side in range(2)] for g in range(PASSES)]
         q_scale = [[keep.tile([P, PAIR * P], U8, name="q_scale%d_%d" % (g, side), align_bytes=64)
@@ -136,18 +134,12 @@ def tile_attend_plq_recomp_topk_kernel(tc, qT, k_words, k_scales, kb, ls, offs, 
             return k_codes
 
         def multiply(g, k_codes):
-            for bank, held in zip(banks, BANKS):
-                width = P if g else held[0][2] - held[0][1]
-                sums = [(place, u, first, at) for place, (u, first, last) in enumerate(held)
-                        for at in range(first, last, width)]
-                for n, (place, u, first, at) in enumerate(sums):
-                    nc.tensor.matmul_mx(
-                        out=bank[:, place, at - first:at - first + width],
-                        lhsT=q_codes[g][u // PAIR][:, u % PAIR * P:(u % PAIR + 1) * P].bitcast(FP8X4),
-                        lhsT_scale=q_scale[g][u // PAIR][:, u % PAIR * P:(u % PAIR + 1) * P],
-                        rhs=k_codes[:, at:at + width].bitcast(FP4X4),
-                        rhs_scale=k_planes[:, g * N + at:g * N + at + width],
-                        start=(g == 0 and n == 0), stop=(g == PASSES - 1 and n == len(sums) - 1))
+            for bank, (u, first) in zip(banks, BANKS):
+                rows = slice(u % PAIR * P, (u % PAIR + 1) * P)
+                nc.tensor.matmul_mx(
+                    out=bank[:], lhsT=q_codes[g][u // PAIR][:, rows].bitcast(FP8X4),
+                    lhsT_scale=q_scale[g][u // PAIR][:, rows], rhs=k_codes[:, first:first + HALF].bitcast(FP4X4),
+                    rhs_scale=k_planes[:, g * N + first:g * N + first + HALF], start=(g == 0), stop=(g == PASSES - 1))
 
         codes0 = part(0)
         codes1 = part(1)
@@ -158,8 +150,9 @@ def tile_attend_plq_recomp_topk_kernel(tc, qT, k_words, k_scales, kb, ls, offs, 
 
         y_rows = out_0.rearrange("(p u) i -> p u i", u=PACK)
         y = keep.tile([P, PACK, N], F32, name="y")
-        steps = [(bank[:, place, :], u, first, last) for bank, held in zip(banks, BANKS)
-                 for place, (u, first, last) in enumerate(held)]
+        steps = [(bank[:, at:at + width], u, first + at, first + at + width)
+                 for b, (bank, (u, first)) in enumerate(zip(banks, BANKS))
+                 for width in (HALF if b else QUARTER,) for at in range(0, HALF, width)]
         for scores, u, first, last in steps:
             z = shared.tile([P, last - first], F32, name="z%d_%d" % (u, first), align_bytes=64,
                             offset=SUM_AT + (u * N + first) * 4)

@@ -35,6 +35,7 @@ STAGE_AT = 3 * RAW
 GROUPED_AT = ((STAGE_AT, STAGE_AT + STAGE), (STAGE_AT + 2 * STAGE, STAGE_AT + 3 * STAGE))
 CODES_AT = (STAGE_AT - 1024, STAGE_AT - 2048)
 SUM_AT = GROUPED_AT[1][1]
+WORD_AT = SUM_AT + PACK * N * 4
 
 
 def tile_attend_plq_recomp_topk_kernel(tc, qT, k_words, k_scales, kb, ls, offs, out_0, out_1, out_2):
@@ -60,7 +61,7 @@ def tile_attend_plq_recomp_topk_kernel(tc, qT, k_words, k_scales, kb, ls, offs, 
         nc.sync.dma_start(scale_words[96:128, :], k_scales.bitcast(I32).rearrange("o f t -> (o f) t"))
         bias_pool = keep.tile([P, T], F32, name="bias_pool", align_bytes=64)
         nc.sync.dma_start(bias_pool[P - 1:P, :], kb[0:1, :])
-        word_pool = keep.tile([P, T], I32, name="word_pool", align_bytes=64)
+        word_pool = shared.tile([P, T], I32, name="word_pool", offset=WORD_AT, align_bytes=64)
         nc.sync.dma_start(word_pool[:], k_words[0].rearrange("p t b -> p (t b)").bitcast(I32))
         q_raw = [load_q(0)]
 
@@ -95,16 +96,22 @@ def tile_attend_plq_recomp_topk_kernel(tc, qT, k_words, k_scales, kb, ls, offs, 
         nc.vector.tensor_copy(k_pairs[:], word_pool[:].bitcast(U32).indirect(offsets[:]))
         halves = k_pairs[:].bitcast(U16).rearrange("p (i h) -> p h i", h=2)
 
+        def part(g):
+            k_codes = shared.tile([P, N], U16, name="k_codes%d" % g, offset=CODES_AT[g], align_bytes=64)
+            nc.vector.tensor_copy(k_codes[:], halves[:, g, :])
+            return k_codes
+
+        codes0 = part(0)
+        codes1 = part(1)
         turned = psum.tile([P, N // P, P], F32, name="turned", offset=6 * BANK)
         for s in range(N // P):
             nc.tensor.transpose(turned[:, s, :], bias_row[:, s * P:(s + 1) * P], ident[:])
-        bias_cols = keep.tile([P, N // P], F32, name="bias_cols", align_bytes=64)
+        bias_cols = shared.tile([P, N // P], F32, name="bias_cols", offset=WORD_AT, align_bytes=64)
         nc.scalar.copy(bias_cols[:], turned[:, :, P - 1])
         spread = psum.tile([P, N], F32, name="spread", offset=7 * BANK)
         for s in range(N // P):
             nc.tensor.transpose(spread[:, s * P:(s + 1) * P], bias_cols[:, s:s + 1].to_broadcast([P, P]), ident[:])
         bias_all = keep.tile([P, N], F32, name="bias_all", align_bytes=64)
-        nc.scalar.copy(bias_all[:], spread[:])
 
         banks = [psum.tile([P, HALF], F32, name="scores%d" % b, offset=b * BANK) for b in range(len(BANKS))]
         q_codes = [[keep.tile([P, PAIR * P], U32, name="q_codes%d_%d" % (g, side), align_bytes=64)
@@ -128,11 +135,6 @@ def tile_attend_plq_recomp_topk_kernel(tc, qT, k_words, k_scales, kb, ls, offs, 
                                       scales=q_scale[g][side][:, a * P:b * P],
                                       in_=grouped[side][:, a:b].rearrange("p u m j -> p (u m j)"))
 
-        def part(g):
-            k_codes = shared.tile([P, N], U16, name="k_codes%d" % g, offset=CODES_AT[g], align_bytes=64)
-            nc.vector.tensor_copy(k_codes[:], halves[:, g, :])
-            return k_codes
-
         def multiply(g, k_codes):
             for bank, (u, first) in zip(banks, BANKS):
                 rows = slice(u % PAIR * P, (u % PAIR + 1) * P)
@@ -141,9 +143,8 @@ def tile_attend_plq_recomp_topk_kernel(tc, qT, k_words, k_scales, kb, ls, offs, 
                     lhsT_scale=q_scale[g][u // PAIR][:, rows], rhs=k_codes[:, first:first + HALF].bitcast(FP4X4),
                     rhs_scale=k_planes[:, g * N + first:g * N + first + HALF], start=(g == 0), stop=(g == PASSES - 1))
 
-        codes0 = part(0)
-        codes1 = part(1)
         quantise(0)
+        nc.scalar.copy(bias_all[:], spread[:])
         multiply(0, codes0)
         quantise(1)
         multiply(1, codes1)

@@ -35,7 +35,6 @@ STAGE_AT = 3 * RAW
 GROUPED_AT = ((STAGE_AT, STAGE_AT + STAGE), (STAGE_AT + 2 * STAGE, STAGE_AT + 3 * STAGE))
 CODES_AT = (STAGE_AT - 1024, STAGE_AT - 2048)
 SUM_AT = GROUPED_AT[1][1]
-WORD_AT = SUM_AT + PACK * N * 4
 
 
 def tile_attend_plq_recomp_topk_kernel(tc, qT, k_words, k_scales, kb, ls, offs, out_0, out_1, out_2):
@@ -60,9 +59,9 @@ def tile_attend_plq_recomp_topk_kernel(tc, qT, k_words, k_scales, kb, ls, offs, 
         scale_words = scale_pool[:].bitcast(I32)
         nc.sync.dma_start(scale_words[96:128, :], k_scales.bitcast(I32).rearrange("o f t -> (o f) t"))
         bias_pool = keep.tile([P, T], F32, name="bias_pool", align_bytes=64)
-        nc.sync.dma_start(bias_pool[P - 1:P, :], kb[0:1, :])
-        word_pool = shared.tile([P, T], I32, name="word_pool", offset=WORD_AT, align_bytes=64)
+        word_pool = keep.tile([P, T], I32, name="word_pool", align_bytes=64)
         nc.sync.dma_start(word_pool[:], k_words[0].rearrange("p t b -> p (t b)").bitcast(I32))
+        nc.sync.dma_start(bias_pool[P - 1:P, :], kb[0:1, :])
         q_raw = [load_q(0)]
 
         nc.gpsimd.memset(scale_words[0:96, :], 0)
@@ -90,8 +89,15 @@ def tile_attend_plq_recomp_topk_kernel(tc, qT, k_words, k_scales, kb, ls, offs, 
         lse = shared.tile([P, PACK], F32, name="lse", offset=LSE_AT, align_bytes=64)
         nc.sync.dma_start(lse[:], ls[0].rearrange("(p u) o -> p (u o)", u=PACK))
 
-        bias_row = keep.tile([P, N], F32, name="bias_row", align_bytes=64)
-        nc.scalar.activation(bias_row[:], bias_pool[:].indirect(offsets[:]), ACT.Copy)
+        minus_lse = keep.tile([P, PACK], F32, name="minus_lse", align_bytes=64)
+        nc.gpsimd.tensor_scalar(minus_lse[:], lse[:], -1.0, 0.0, ALU.mult, ALU.add)
+
+        bias_rows = []
+        for h in range(2):
+            bias_row = keep.tile([P, HALF], F32, name="bias_row%d" % h, align_bytes=64)
+            nc.scalar.activation(bias_row[:], bias_pool[:].indirect(offsets[:, h * HALF // 16:(h + 1) * HALF // 16]),
+                                 ACT.Copy)
+            bias_rows.append(bias_row)
         k_pairs = keep.tile([P, N], U32, name="k_pairs", align_bytes=64)
         nc.vector.tensor_copy(k_pairs[:], word_pool[:].bitcast(U32).indirect(offsets[:]))
         halves = k_pairs[:].bitcast(U16).rearrange("p (i h) -> p h i", h=2)
@@ -105,8 +111,8 @@ def tile_attend_plq_recomp_topk_kernel(tc, qT, k_words, k_scales, kb, ls, offs, 
         codes1 = part(1)
         turned = psum.tile([P, N // P, P], F32, name="turned", offset=6 * BANK)
         for s in range(N // P):
-            nc.tensor.transpose(turned[:, s, :], bias_row[:, s * P:(s + 1) * P], ident[:])
-        bias_cols = shared.tile([P, N // P], F32, name="bias_cols", offset=WORD_AT, align_bytes=64)
+            nc.tensor.transpose(turned[:, s, :], bias_rows[s // 2][:, s % 2 * P:(s % 2 + 1) * P], ident[:])
+        bias_cols = keep.tile([P, N // P], F32, name="bias_cols", align_bytes=64)
         nc.scalar.copy(bias_cols[:], turned[:, :, P - 1])
         spread = psum.tile([P, N], F32, name="spread", offset=7 * BANK)
         for s in range(N // P):
@@ -157,9 +163,8 @@ def tile_attend_plq_recomp_topk_kernel(tc, qT, k_words, k_scales, kb, ls, offs, 
         for scores, u, first, last in steps:
             z = shared.tile([P, last - first], F32, name="z%d_%d" % (u, first), align_bytes=64,
                             offset=SUM_AT + (u * N + first) * 4)
-            nc.vector.scalar_tensor_tensor(z[:], scores, lse[:, u:u + 1], bias_all[:, first:last],
-                                           ALU.subtract, ALU.add)
-            nc.scalar.activation(y[:, u, first:last], z[:], ACT.Exp)
+            nc.vector.tensor_tensor(z[:], scores, bias_all[:, first:last], ALU.add)
+            nc.scalar.activation(y[:, u, first:last], z[:], ACT.Exp, bias=minus_lse[:, u:u + 1])
             if last == N:
                 nc.sync.dma_start(y_rows[:, u:u + 1, :], y[:, u:u + 1, :])
 

@@ -26,6 +26,8 @@ BANK = 2048
 QUARTER = N // 4
 BANKS = ((0, 0), (0, HALF), (1, 0), (1, HALF), (2, 0), (3, 0), (2, HALF), (3, HALF))
 PIECES = ((0, 0, 128, 84, 76), (1, 0, 128, 84, 68))
+STEPS = ((0, 0, 128), (0, 128, 256), (0, 256, 512), (1, 0, 256), (1, 256, 512), (2, 0, 256), (3, 0, 128),
+         (2, 256, 512), (3, 128, 256), (3, 256, 512))
 RAW = PACK * NQ * 4
 STAGE = PAIR * P * PACK * 2
 RAW_AT = (0, RAW + T // 2 + 64)
@@ -157,9 +159,8 @@ def tile_attend_plq_recomp_topk_kernel(tc, qT, k_words, k_scales, kb, ls, offs, 
 
         y_rows = out_0.rearrange("(p u) i -> p u i", u=PACK)
         y = keep.tile([P, PACK, N], F32, name="y")
-        steps = [(bank[:, at:at + width], u, first + at, first + at + width)
-                 for b, (bank, (u, first)) in enumerate(zip(banks, BANKS))
-                 for width in (HALF if b else QUARTER,) for at in range(0, HALF, width)]
+        steps = [(banks[BANKS.index((u, first - first % HALF))][:, first % HALF:first % HALF + last - first],
+                  u, first, last) for u, first, last in STEPS]
         for scores, u, first, last in steps:
             z = shared.tile([P, last - first], F32, name="z%d_%d" % (u, first), align_bytes=64,
                             offset=SUM_AT + (u * N + first) * 4)
@@ -175,8 +176,9 @@ def tile_attend_plq_recomp_topk_kernel(tc, qT, k_words, k_scales, kb, ls, offs, 
         woven = []
         for first, last, engine in pieces:
             piece = keep.tile([P, last - first, PACK], BF16, name="woven%d" % first, align_bytes=64)
-            engine(piece[:].rearrange("p (c k) u -> p c u k", k=4),
-                   y[:, :, first:last].rearrange("p u (c k) -> p c u k", k=4))
+            for at in range(first, last, QUARTER):
+                engine(piece[:, at - first:at - first + QUARTER].rearrange("p (c k) u -> p c u k", k=4),
+                       y[:, :, at:at + QUARTER].rearrange("p u (c k) -> p c u k", k=4))
             woven.append(piece)
         for (first, last, engine), piece in zip(pieces, woven):
             nc.vector.quantize_mx(out=y_codes[:, first:last].bitcast(FP8X4), scales=y_scale[:, first:last],

@@ -25,7 +25,7 @@ PAIR = 2
 BANK = 2048
 QUARTER = N // 4
 BANKS = ((0, 0), (0, HALF), (1, 0), (1, HALF), (2, 0), (3, 0), (2, HALF), (3, HALF))
-PIECES = ((0, 0, 128, 84, 76), (1, 0, 128, 84, 68))
+PIECES = ((0, 0, 128, 84, 76), (1, 0, 128, 76, 60))
 STEPS = ((0, 0, 128), (0, 128, 256), (0, 256, 512), (1, 0, 256), (1, 256, 512), (2, 0, 256), (3, 0, 128),
          (2, 256, 512), (3, 128, 256), (3, 256, 512))
 RAW = PACK * NQ * 4
@@ -36,7 +36,8 @@ SCALE_AT = LSE_AT - T // 2
 STAGE_AT = 3 * RAW
 GROUPED_AT = ((STAGE_AT, STAGE_AT + STAGE), (STAGE_AT + 2 * STAGE, STAGE_AT + 3 * STAGE))
 CODES_AT = (STAGE_AT - 1024, STAGE_AT - 2048)
-SUM_AT = GROUPED_AT[1][1]
+SUM_AT = STAGE_AT + 4 * STAGE
+EARLY_STEPS = 3
 
 
 def tile_attend_plq_recomp_topk_kernel(tc, qT, k_words, k_scales, kb, ls, offs, out_0, out_1, out_2):
@@ -91,9 +92,6 @@ def tile_attend_plq_recomp_topk_kernel(tc, qT, k_words, k_scales, kb, ls, offs, 
         lse = shared.tile([P, PACK], F32, name="lse", offset=LSE_AT, align_bytes=64)
         nc.sync.dma_start(lse[:], ls[0].rearrange("(p u) o -> p (u o)", u=PACK))
 
-        minus_lse = keep.tile([P, PACK], F32, name="minus_lse", align_bytes=64)
-        nc.gpsimd.tensor_scalar(minus_lse[:], lse[:], -1.0, 0.0, ALU.mult, ALU.add)
-
         bias_rows = []
         for h in range(2):
             bias_row = keep.tile([P, HALF], F32, name="bias_row%d" % h, align_bytes=64)
@@ -127,7 +125,7 @@ def tile_attend_plq_recomp_topk_kernel(tc, qT, k_words, k_scales, kb, ls, offs, 
         q_scale = [[keep.tile([P, PAIR * P], U8, name="q_scale%d_%d" % (g, side), align_bytes=64)
                     for side in range(2)] for g in range(PASSES)]
 
-        def quantise(piece):
+        def cast(piece):
             g, m0, m1 = PIECES[piece][:3]
             grouped = [shared.tile([P, PAIR, m1 - m0, PACK], BF16, name="grouped%d_%d" % (piece, side),
                                    align_bytes=64, offset=GROUPED_AT[piece][side]) for side in range(2)]
@@ -138,30 +136,42 @@ def tile_attend_plq_recomp_topk_kernel(tc, qT, k_words, k_scales, kb, ls, offs, 
                     if a < b:
                         engine(grouped[side][:].rearrange("p u m j -> p m j u")[:, a:b],
                                by_group[:, a:b, :, side * PAIR:(side + 1) * PAIR])
-            for side, a, b in ((0, 0, 1), (0, 1, 2), (1, 0, 2)):
+            return grouped
+
+        def quantise(g, grouped, side):
+            for a, b in (((0, 1), (1, 2)), ((0, 2),))[side]:
                 nc.vector.quantize_mx(out=q_codes[g][side][:, a * P:b * P].bitcast(FP8X4),
                                       scales=q_scale[g][side][:, a * P:b * P],
                                       in_=grouped[side][:, a:b].rearrange("p u m j -> p (u m j)"))
 
-        def multiply(g, k_codes):
-            for bank, (u, first) in zip(banks, BANKS):
+        def multiply(g, k_codes, side):
+            for bank, (u, first) in list(zip(banks, BANKS))[4 * side:4 * side + 4]:
                 rows = slice(u % PAIR * P, (u % PAIR + 1) * P)
                 nc.tensor.matmul_mx(
                     out=bank[:], lhsT=q_codes[g][u // PAIR][:, rows].bitcast(FP8X4),
                     lhsT_scale=q_scale[g][u // PAIR][:, rows], rhs=k_codes[:, first:first + HALF].bitcast(FP4X4),
                     rhs_scale=k_planes[:, g * N + first:g * N + first + HALF], start=(g == 0), stop=(g == PASSES - 1))
 
-        quantise(0)
+        grouped0 = cast(0)
+        quantise(0, grouped0, 0)
+        quantise(0, grouped0, 1)
         nc.scalar.copy(bias_all[:], spread[:])
-        multiply(0, codes0)
-        quantise(1)
-        multiply(1, codes1)
+        multiply(0, codes0, 0)
+        multiply(0, codes0, 1)
+        grouped1 = cast(1)
+        quantise(1, grouped1, 0)
+        minus_lse = keep.tile([P, PACK], F32, name="minus_lse", align_bytes=64)
+        nc.scalar.mul(minus_lse[:], lse[:], -1.0)
+        multiply(1, codes1, 0)
 
         y_rows = out_0.rearrange("(p u) i -> p u i", u=PACK)
         y = keep.tile([P, PACK, N], F32, name="y")
         steps = [(banks[BANKS.index((u, first - first % HALF))][:, first % HALF:first % HALF + last - first],
                   u, first, last) for u, first, last in STEPS]
-        for scores, u, first, last in steps:
+        for step, (scores, u, first, last) in enumerate(steps):
+            if step == EARLY_STEPS:
+                quantise(1, grouped1, 1)
+                multiply(1, codes1, 1)
             z = shared.tile([P, last - first], F32, name="z%d_%d" % (u, first), align_bytes=64,
                             offset=SUM_AT + (u * N + first) * 4)
             nc.vector.tensor_tensor(z[:], scores, bias_all[:, first:last], ALU.add)

@@ -26,8 +26,9 @@ BANK = 2048
 QUARTER = N // 4
 BANKS = ((0, 0), (0, HALF), (1, 0), (1, HALF), (2, 0), (3, 0), (2, HALF), (3, HALF))
 PIECES = ((0, 0, 128, 84, 76), (1, 0, 128, 76, 60))
-STEPS = ((0, 0, 128), (0, 128, 256), (0, 256, 512), (1, 0, 256), (1, 256, 512), (2, 0, 256), (3, 0, 128),
-         (2, 256, 512), (3, 128, 256), (3, 256, 512))
+STEPS = ((0, 0, 128), (0, 128, 256), (0, 256, 512), (1, 0, 256), (1, 256, 512), (2, 0, 256), (3, 0, 256),
+         (2, 256, 512), (3, 256, 512))
+STORES = {1: (0, 256), 3: (256, 768), 5: (768, 1280), 8: (1280, 2048)}
 RAW = PACK * NQ * 4
 STAGE = PAIR * P * PACK * 2
 RAW_AT = (0, RAW + T // 2 + 64)
@@ -164,7 +165,7 @@ def tile_attend_plq_recomp_topk_kernel(tc, qT, k_words, k_scales, kb, ls, offs, 
         nc.scalar.mul(minus_lse[:], lse[:], -1.0)
         multiply(1, codes1, 0)
 
-        y_rows = out_0.rearrange("(p u) i -> p u i", u=PACK)
+        y_rows = out_0.rearrange("(p u) i -> p (u i)", u=PACK)
         y = keep.tile([P, PACK, N], F32, name="y")
         steps = [(banks[BANKS.index((u, first - first % HALF))][:, first % HALF:first % HALF + last - first],
                   u, first, last) for u, first, last in STEPS]
@@ -176,8 +177,9 @@ def tile_attend_plq_recomp_topk_kernel(tc, qT, k_words, k_scales, kb, ls, offs, 
                             offset=SUM_AT + (u * N + first) * 4)
             nc.vector.tensor_tensor(z[:], scores, bias_all[:, first:last], ALU.add)
             nc.scalar.activation(y[:, u, first:last], z[:], ACT.Exp, bias=minus_lse[:, u:u + 1])
-            if last == N:
-                nc.sync.dma_start(y_rows[:, u:u + 1, :], y[:, u:u + 1, :])
+            if step in STORES:
+                since, until = STORES[step]
+                nc.sync.dma_start(y_rows[:, since:until], y[:].rearrange("p u i -> p (u i)")[:, since:until])
 
         y_scale = keep.tile([P, N], U8, name="y_scale", align_bytes=64)
         y_codes = keep.tile([P, N], I32, name="y_codes", align_bytes=64)
@@ -186,9 +188,8 @@ def tile_attend_plq_recomp_topk_kernel(tc, qT, k_words, k_scales, kb, ls, offs, 
         woven = []
         for first, last, engine in pieces:
             piece = keep.tile([P, last - first, PACK], BF16, name="woven%d" % first, align_bytes=64)
-            for at in range(first, last, QUARTER):
-                engine(piece[:, at - first:at - first + QUARTER].rearrange("p (c k) u -> p c u k", k=4),
-                       y[:, :, at:at + QUARTER].rearrange("p u (c k) -> p c u k", k=4))
+            engine(piece[:].rearrange("p (c k) u -> p c u k", k=4),
+                   y[:, :, first:last].rearrange("p u (c k) -> p c u k", k=4))
             woven.append(piece)
         for (first, last, engine), piece in zip(pieces, woven):
             nc.vector.quantize_mx(out=y_codes[:, first:last].bitcast(FP8X4), scales=y_scale[:, first:last],

@@ -25,7 +25,7 @@ PAIR = 2
 BANK = 2048
 QUARTER = N // 4
 BANKS = ((0, 0), (0, HALF), (1, 0), (1, HALF), (2, 0), (3, 0), (2, HALF), (3, HALF))
-PIECES = ((0, 0, 128, 84, 76), (1, 0, 128, 76, 60))
+PIECES = ((0, 0, 128, 84, 76), (1, 0, 128, 76, 68))
 STEPS = ((0, 0, 128), (0, 128, 256), (0, 256, 512), (1, 0, 256), (1, 256, 512), (2, 0, 256), (3, 0, 256),
          (2, 256, 512), (3, 256, 512))
 STORES = {1: (0, 256), 3: (256, 768), 5: (768, 1280), 8: (1280, 2048)}

from contextlib import ExitStack

import concourse.mybir as mybir
from concourse.masks import make_identity

F32 = mybir.dt.float32
BF16 = mybir.dt.bfloat16
I32 = mybir.dt.int32
U32 = mybir.dt.uint32
U16 = mybir.dt.uint16
U8 = mybir.dt.uint8
FP8X4 = mybir.dt.float8_e4m3fn_x4
FP4X4 = mybir.dt.float4_e2m1fn_x4
ACT = mybir.ActivationFunctionType
ALU = mybir.AluOpType

P = 128
PACK = 4
N, T, D, NQ = 512, 2048, 1024, 512
PASSES = D // (P * PACK)
FLOPS = 2 * NQ * N * D

HALF = N // 2
PAIR = 2
BANK = 2048
QUARTER = N // 4
BANKS = ((0, 0), (0, HALF), (1, 0), (1, HALF), (2, 0), (3, 0), (2, HALF), (3, HALF))
PIECES = ((0, 0, 128, 84, 76), (1, 0, 128, 76, 68))
STEPS = ((0, 0, 128), (0, 128, 256), (0, 256, 512), (1, 0, 256), (1, 256, 512), (2, 0, 256), (3, 0, 256),
         (2, 256, 512), (3, 256, 512))
STORES = {1: (0, 256), 3: (256, 768), 5: (768, 1280), 8: (1280, 2048)}
RAW = PACK * NQ * 4
STAGE = PAIR * P * PACK * 2
RAW_AT = (0, RAW + T // 2 + 64)
LSE_AT = RAW + T // 2
SCALE_AT = LSE_AT - T // 2
STAGE_AT = 3 * RAW
GROUPED_AT = ((STAGE_AT, STAGE_AT + STAGE), (STAGE_AT + 2 * STAGE, STAGE_AT + 3 * STAGE))
CODES_AT = (STAGE_AT - 1024, STAGE_AT - 2048)
SUM_AT = STAGE_AT + 4 * STAGE
EARLY_STEPS = 3


def tile_attend_plq_recomp_topk_kernel(tc, qT, k_words, k_scales, kb, ls, offs, out_0, out_1, out_2):
    nc = tc.nc
    with ExitStack() as ctx:
        keep = ctx.enter_context(tc.tile_pool(name="keep", bufs=1))
        shared = ctx.enter_context(tc.tile_pool(name="shared", bufs=1))
        psum = ctx.enter_context(tc.psum_pool(name="psum", bufs=1))

        q_rows = qT[0].rearrange("(g p j) q -> g p j q", g=PASSES, j=PACK)

        def load_q(piece):
            g, m0, m1 = PIECES[piece][:3]
            raw = shared.tile([P, PACK, PACK * (m1 - m0)], F32, name="q_raw%d" % piece, offset=RAW_AT[piece],
                              align_bytes=64)
            nc.sync.dma_start(raw[:], q_rows[g, :, :, PACK * m0:PACK * m1])
            return raw

        offsets = keep.tile([P, N // 16], U16, name="offsets")
        nc.sync.dma_start(offsets[:], offs)
        scale_pool = shared.tile([P, T], U8, name="scale_pool", offset=SCALE_AT, align_bytes=64)
        scale_words = scale_pool[:].bitcast(I32)
        nc.sync.dma_start(scale_words[96:128, :], k_scales.bitcast(I32).rearrange("o f t -> (o f) t"))
        bias_pool = keep.tile([P, T], F32, name="bias_pool", align_bytes=64)
        word_pool = keep.tile([P, T], I32, name="word_pool", align_bytes=64)
        nc.sync.dma_start(word_pool[:], k_words[0].rearrange("p t b -> p (t b)").bitcast(I32))
        nc.sync.dma_start(bias_pool[P - 1:P, :], kb[0:1, :])
        q_raw = [load_q(0)]

        nc.gpsimd.memset(scale_words[0:96, :], 0)
        warm_in = keep.tile([P, 1], F32, name="warm_in")
        warm_out = keep.tile([P, 1], F32, name="warm_out")
        nc.gpsimd.memset(warm_in[:], 0.0)
        nc.scalar.activation(warm_out[:], warm_in[:], ACT.Exp)
        k_planes = keep.tile([P, PASSES * N], U8, name="k_planes", align_bytes=64)
        nc.gpsimd.memset(k_planes[:].bitcast(I32), 0)
        ident = keep.tile([P, P], F32, name="ident")
        make_identity(nc, ident[:])
        nc.vector.memset(bias_pool[0:P - 1, :], 0.0)

        k_rows = keep.tile([P, N], U8, name="k_rows", align_bytes=64)
        nc.vector.tensor_copy(k_rows[:], scale_pool[:].indirect(offsets[:]))

        def move_plane(g):
            for r in range(4):
                nc.sync.dma_start(k_planes[:, g * N:(g + 1) * N].bitcast(I32)[r:P:32, :],
                                  k_rows[:].bitcast(I32)[96 + 16 * g + r:96 + 16 * (g + 1):4, :])

        move_plane(0)
        q_raw.append(load_q(1))
        move_plane(1)
        lse = shared.tile([P, PACK], F32, name="lse", offset=LSE_AT, align_bytes=64)
        nc.sync.dma_start(lse[:], ls[0].rearrange("(p u) o -> p (u o)", u=PACK))

        bias_rows = []
        for h in range(2):
            bias_row = keep.tile([P, HALF], F32, name="bias_row%d" % h, align_bytes=64)
            nc.scalar.activation(bias_row[:], bias_pool[:].indirect(offsets[:, h * HALF // 16:(h + 1) * HALF // 16]),
                                 ACT.Copy)
            bias_rows.append(bias_row)
        k_pairs = keep.tile([P, N], U32, name="k_pairs", align_bytes=64)
        nc.vector.tensor_copy(k_pairs[:], word_pool[:].bitcast(U32).indirect(offsets[:]))
        halves = k_pairs[:].bitcast(U16).rearrange("p (i h) -> p h i", h=2)

        def part(g):
            k_codes = shared.tile([P, N], U16, name="k_codes%d" % g, offset=CODES_AT[g], align_bytes=64)
            nc.vector.tensor_copy(k_codes[:], halves[:, g, :])
            return k_codes

        codes0 = part(0)
        codes1 = part(1)
        turned = psum.tile([P, N // P, P], F32, name="turned", offset=6 * BANK)
        for s in range(N // P):
            nc.tensor.transpose(turned[:, s, :], bias_rows[s // 2][:, s % 2 * P:(s % 2 + 1) * P], ident[:])
        bias_cols = keep.tile([P, N // P], F32, name="bias_cols", align_bytes=64)
        nc.scalar.copy(bias_cols[:], turned[:, :, P - 1])
        spread = psum.tile([P, N], F32, name="spread", offset=7 * BANK)
        for s in range(N // P):
            nc.tensor.transpose(spread[:, s * P:(s + 1) * P], bias_cols[:, s:s + 1].to_broadcast([P, P]), ident[:])
        bias_all = keep.tile([P, N], F32, name="bias_all", align_bytes=64)

        banks = [psum.tile([P, HALF], F32, name="scores%d" % b, offset=b * BANK) for b in range(len(BANKS))]
        q_codes = [[keep.tile([P, PAIR * P], U32, name="q_codes%d_%d" % (g, side), align_bytes=64)
                    for side in range(2)] for g in range(PASSES)]
        q_scale = [[keep.tile([P, PAIR * P], U8, name="q_scale%d_%d" % (g, side), align_bytes=64)
                    for side in range(2)] for g in range(PASSES)]

        def cast(piece):
            g, m0, m1 = PIECES[piece][:3]
            grouped = [shared.tile([P, PAIR, m1 - m0, PACK], BF16, name="grouped%d_%d" % (piece, side),
                                   align_bytes=64, offset=GROUPED_AT[piece][side]) for side in range(2)]
            by_group = q_raw[piece][:].rearrange("p j (m u) -> p m j u", u=PACK)
            for side in range(2):
                share = PIECES[piece][3 + side]
                for engine, a, b in ((nc.vector.tensor_copy, 0, share), (nc.scalar.copy, share, m1 - m0)):
                    if a < b:
                        engine(grouped[side][:].rearrange("p u m j -> p m j u")[:, a:b],
                               by_group[:, a:b, :, side * PAIR:(side + 1) * PAIR])
            return grouped

        def quantise(g, grouped, side):
            for a, b in (((0, 1), (1, 2)), ((0, 2),))[side]:
                nc.vector.quantize_mx(out=q_codes[g][side][:, a * P:b * P].bitcast(FP8X4),
                                      scales=q_scale[g][side][:, a * P:b * P],
                                      in_=grouped[side][:, a:b].rearrange("p u m j -> p (u m j)"))

        def multiply(g, k_codes, side):
            for bank, (u, first) in list(zip(banks, BANKS))[4 * side:4 * side + 4]:
                rows = slice(u % PAIR * P, (u % PAIR + 1) * P)
                nc.tensor.matmul_mx(
                    out=bank[:], lhsT=q_codes[g][u // PAIR][:, rows].bitcast(FP8X4),
                    lhsT_scale=q_scale[g][u // PAIR][:, rows], rhs=k_codes[:, first:first + HALF].bitcast(FP4X4),
                    rhs_scale=k_planes[:, g * N + first:g * N + first + HALF], start=(g == 0), stop=(g == PASSES - 1))

        grouped0 = cast(0)
        quantise(0, grouped0, 0)
        quantise(0, grouped0, 1)
        nc.scalar.copy(bias_all[:], spread[:])
        multiply(0, codes0, 0)
        multiply(0, codes0, 1)
        grouped1 = cast(1)
        quantise(1, grouped1, 0)
        minus_lse = keep.tile([P, PACK], F32, name="minus_lse", align_bytes=64)
        nc.scalar.mul(minus_lse[:], lse[:], -1.0)
        multiply(1, codes1, 0)

        y_rows = out_0.rearrange("(p u) i -> p (u i)", u=PACK)
        y = keep.tile([P, PACK, N], F32, name="y")
        steps = [(banks[BANKS.index((u, first - first % HALF))][:, first % HALF:first % HALF + last - first],
                  u, first, last) for u, first, last in STEPS]
        for step, (scores, u, first, last) in enumerate(steps):
            if step == EARLY_STEPS:
                quantise(1, grouped1, 1)
                multiply(1, codes1, 1)
            z = shared.tile([P, last - first], F32, name="z%d_%d" % (u, first), align_bytes=64,
                            offset=SUM_AT + (u * N + first) * 4)
            nc.vector.tensor_tensor(z[:], scores, bias_all[:, first:last], ALU.add)
            nc.scalar.activation(y[:, u, first:last], z[:], ACT.Exp, bias=minus_lse[:, u:u + 1])
            if step in STORES:
                since, until = STORES[step]
                nc.sync.dma_start(y_rows[:, since:until], y[:].rearrange("p u i -> p (u i)")[:, since:until])

        y_scale = keep.tile([P, N], U8, name="y_scale", align_bytes=64)
        y_codes = keep.tile([P, N], I32, name="y_codes", align_bytes=64)
        words_out = out_1[0].rearrange("p i b -> p (i b)").bitcast(I32)
        pieces = ((0, 256, nc.vector.tensor_copy), (256, 384, nc.vector.tensor_copy), (384, 512, nc.scalar.copy))
        woven = []
        for first, last, engine in pieces:
            piece = keep.tile([P, last - first, PACK], BF16, name="woven%d" % first, align_bytes=64)
            engine(piece[:].rearrange("p (c k) u -> p c u k", k=4),
                   y[:, :, first:last].rearrange("p u (c k) -> p c u k", k=4))
            woven.append(piece)
        for (first, last, engine), piece in zip(pieces, woven):
            nc.vector.quantize_mx(out=y_codes[:, first:last].bitcast(FP8X4), scales=y_scale[:, first:last],
                                  in_=piece[:].rearrange("p i u -> p (i u)"))
            if last % HALF == 0:
                nc.sync.dma_start(words_out[:, last - HALF:last], y_codes[:, last - HALF:last])
        scales_out = out_2[0].bitcast(I32)
        for quad in range(4):
            queue = nc.sync if quad < 2 else nc.scalar
            queue.dma_start(scales_out[4 * quad:4 * quad + 4, :], y_scale[:].bitcast(I32)[32 * quad:32 * quad + 4, :])
